import numpy as np
import ml_dtypes


def mxq(x, axis, fmt="e4m3"):
    dtype, down = {"e4m3": (ml_dtypes.float8_e4m3fn, 7), "e5m2": (ml_dtypes.float8_e5m2, 14)}[fmt]
    v = np.moveaxis(np.asarray(x, np.float32).astype(ml_dtypes.bfloat16).astype(np.float64), axis, -1)
    blocks = v.reshape(v.shape[:-1] + (-1, 32))
    amax = np.abs(blocks).max(-1, keepdims=True)
    byte = np.maximum(np.where(amax > 0, np.frexp(amax)[1] - 1 + 127, 0) - down, 1)
    scale = np.exp2(byte - 127.0)
    codes = (blocks / scale).astype(np.float32).astype(dtype).astype(np.float64)
    return np.moveaxis((codes * scale).reshape(v.shape), -1, axis)


WIDE = False


def mx_kscale(k):
    if not WIDE:
        return np.ones(k)
    levels = np.array([10, -10, 5, -5, 0])
    if k % 512:
        return np.exp2(np.random.permutation(np.resize(levels, k // 32))).repeat(32)
    a = np.empty((k // 512, 16))
    for p in range(k // 512):
        a[p, :8] = np.random.permutation(np.resize(levels, 8))
        for g in range(8):
            far = levels[np.abs(levels - a[p, g]) >= 10]
            a[p, g + 8] = far[np.random.randint(len(far))]
    return np.exp2(a.ravel()).repeat(32)


def f64(x):
    return np.asarray(x).astype(np.float64)


def striped(idx):
    return np.tile(idx.reshape(-1, 16).T, (8, 1)).astype(np.uint16)


def unstriped(offs):
    return offs[:16].T.reshape(-1).astype(np.int64)


E2M1 = np.array([0.0, 0.5, 1.0, 1.5, 2.0, 3.0, 4.0, 6.0, -0.0, -0.5, -1.0, -1.5, -2.0, -3.0, -4.0, -6.0])


def pack_weight(w, fmt):
    k, n = w.shape
    w = f64(np.asarray(w, np.float32).astype(ml_dtypes.bfloat16)).reshape(k // 32, 32, n)
    amax = np.abs(w).max(1)
    if fmt == "e4m3":
        byte = np.frexp(amax)[1] - 1 + 127 - 7
    else:
        mant, ex = np.frexp(amax / 6.0)
        byte = np.where(mant > 0.5, ex, ex - 1) + 127
    byte = np.clip(np.where(amax > 0, byte, 1), 1, 254)
    scaled = (w * np.exp2(127.0 - byte)[:, None, :]).reshape(k, n).astype(np.float32)
    by_word = np.ascontiguousarray(scaled.reshape(k // 512, 128, 4, n).transpose(0, 1, 3, 2))
    if fmt == "e4m3":
        words = by_word.astype(ml_dtypes.float8_e4m3fn).view(np.uint8)
    else:
        c = by_word.astype(ml_dtypes.float4_e2m1fn).view(np.uint8) & 0xF
        words = (c[..., 0::2] | (c[..., 1::2] << 4)).reshape(k // 512, 128, 2 * n)
    return np.ascontiguousarray(words), np.ascontiguousarray(byte.astype(np.uint8).reshape(k // 512, 16, n))


def unpack_weight(words, scales, fmt):
    g, _, n = scales.shape
    words = np.ascontiguousarray(words).reshape(g, 128, n, -1)
    if fmt == "e4m3":
        vals = words.view(ml_dtypes.float8_e4m3fn).astype(np.float64)
    else:
        nib = np.empty((g, 128, n, 4), np.uint8)
        nib[..., 0::2] = words & 0xF
        nib[..., 1::2] = words >> 4
        vals = E2M1[nib]
    vals = vals * np.repeat(np.exp2(scales.astype(np.float64) - 127.0), 8, axis=1)[..., None]
    return vals.transpose(0, 1, 3, 2).reshape(g * 512, n)


def gelu(v):
    return 0.5 * v * (1.0 + np.tanh(np.sqrt(2.0 / np.pi) * (v + 0.044715 * v**3)))


K, K2, T, T2, S, P, H, N = 1024, 512, 4096, 2048, 1024, 1024, 1024, 256

def setup_inputs():
    n = np.random.standard_normal
    s = mx_kscale(K)[:, None]
    s2 = mx_kscale(K2)[:, None]
    u = mx_kscale(H)[:, None]
    tab_words, tab_scales = pack_weight(n((K, T)) * s, "e4m3")
    w4_words, w4_scales = pack_weight(1.5 * n((K, H)) / np.sqrt(K) / s, "e2m1")
    return {
        "tab_words": tab_words, "tab_scales": tab_scales,
        "w4_words": w4_words, "w4_scales": w4_scales,
        "base": (n((K2, T2)) * s2).astype(np.float32),
        "xs": (np.round(16 * n((K2, S))) / 16 * s2).astype(np.float32),
        "w1": (1.5 * n((K2, H)) / np.sqrt(K2) / s2).astype(np.float32),
        "gain": (np.random.uniform(0.5, 1.5, H) * u[:, 0]).astype(np.float32),
        "wf": (1.5 * n((H, N)) / np.sqrt(H) / u).astype(np.float32),
        "thr": np.random.uniform(0.5, 1.5, N).astype(np.float32),
        "offs": striped(np.random.permutation(T)[:P]),
        "offs2": striped(np.random.permutation(T2)[:S]),
        "offs3": striped(np.random.permutation(T2)[:P]),
    }

def reference(tab_words, tab_scales, w4_words, w4_scales, base, xs, w1, gain, wf, thr, offs, offs2, offs3):
    page = f64(base).copy()
    page[:, unstriped(offs2)] = f64(xs)
    a = mxq(f64(w1), 0, "e4m3").T @ mxq(page, 0, "e4m3")
    v = unpack_weight(tab_words, tab_scales, "e4m3")[:, unstriped(offs)]
    b = unpack_weight(w4_words, w4_scales, "e2m1").T @ v
    both = np.concatenate([a[:, unstriped(offs3)], b], axis=1)
    e = np.square(both) + 1.0
    z = np.log(e[:, :P] / e[:, P:]) * f64(gain)[:, None]
    y = mxq(f64(wf), 0, "e4m3").T @ mxq(z, 0, "e4m3")
    return y - f64(thr)[:, None]

@@ -1,0 +1,352 @@
+from contextlib import ExitStack
+
+import concourse.mybir as mybir
+from concourse.masks import make_identity
+
+K, K2, T, T2, S, NP, H, N = 1024, 512, 4096, 2048, 1024, 1024, 1024, 256
+FLOPS = 2 * (K2 * H * T2 + K * H * NP + H * N * NP)
+
+F32 = mybir.dt.float32
+BF16 = mybir.dt.bfloat16
+I32 = mybir.dt.int32
+U32 = mybir.dt.uint32
+U16 = mybir.dt.uint16
+U8 = mybir.dt.uint8
+FP8X4 = mybir.dt.float8_e4m3fn_x4
+FP4X4 = mybir.dt.float4_e2m1fn_x4
+ACT = mybir.ActivationFunctionType
+ALU = mybir.AluOpType
+
+P = 128
+BANK = 512
+SCATTER_ORDER = (0, 2, 3, 1)
+ON_VECTOR = ((0, 3), (1, 3), (2, 3), (3, 3), (4, 3))
+
+
+def tile_list_gnss_spoofing_monitor_kernel(
+    tc, tab_words, tab_scales, w4_words, w4_scales, base, xs, w1, gain, wf, thr, offs, offs2, offs3, out
+):
+    nc = tc.nc
+    with ExitStack() as ctx:
+        lists = ctx.enter_context(tc.tile_pool(name="lists", bufs=1))
+        keep = ctx.enter_context(tc.tile_pool(name="keep", bufs=1))
+        psum = ctx.enter_context(tc.psum_pool(name="psum", bufs=8))
+
+        def gp_cast(dst, src):
+            nc.gpsimd.tensor_scalar(dst, src, 1.0, 0.0, ALU.mult, ALU.add)
+
+        tab_list = lists.tile([P, NP // 16], U16, name="tab_list")
+        fresh_list = lists.tile([P, S // 16], U16, name="fresh_list")
+        suspect_list = lists.tile([P, NP // 16], U16, name="suspect_list")
+        tab_sc = keep.tile([P, T], U8, name="tab_sc", align_bytes=64)
+        nc.gpsimd.memset(tab_sc[:].bitcast(I32), 0)
+        w4_sc_raw = keep.tile([P, 2, H], U8, name="w4_sc_raw", align_bytes=64)
+        nc.vector.memset(w4_sc_raw[:].bitcast(I32), 0)
+        nc.sync.dma_start(tab_list[:], offs)
+        for quad in range(4):
+            nc.sync.dma_start(
+                tab_sc[32 * quad : 32 * quad + 8, :].bitcast(I32),
+                tab_scales[:, 4 * quad : 4 * quad + 4, :].bitcast(I32),
+            )
+
+        base_planes = base.rearrange("(p t) c -> t p c", t=4)
+        xs_planes = xs.rearrange("(p t) c -> t p c", t=4)
+        page = {}
+        fresh = {}
+
+        def load_plane(t, pieces=1):
+            page[t] = keep.tile([P, T2], F32, name="page%d" % t, align_bytes=64)
+            fresh[t] = keep.tile([P, S], F32, name="fresh%d" % t, tag="fresh%d" % t, align_bytes=64)
+            for dst, src, width in ((page[t], base_planes[t], T2 // pieces), (fresh[t], xs_planes[t], S // pieces)):
+                for i in range(pieces):
+                    nc.sync.dma_start(dst[:, width * i : width * (i + 1)], src[:, width * i : width * (i + 1)])
+
+        tab_w = []
+
+        def load_table(a):
+            tw = keep.tile([P, T], U32, name="tab_w%d" % a, tag="sixteen", bufs=2, align_bytes=64)
+            words = tab_words[a].rearrange("p t i -> p (t i)").bitcast(I32)
+            for half in range(2):
+                cols = slice(T // 2 * half, T // 2 * (half + 1))
+                nc.sync.dma_start(tw[:, cols].bitcast(I32), words[:, cols])
+            tab_w.append(tw)
+
+        load_table(0)
+        for quad in range(4):
+            nc.sync.dma_start(
+                w4_sc_raw[32 * quad : 32 * quad + 4, :, :].bitcast(I32),
+                w4_scales[:, 4 * quad : 4 * quad + 4, :].bitcast(I32).rearrange("a r w -> r a w"),
+            )
+        w4_raw = keep.tile([P, 2, 2 * H], U8, name="w4_raw", align_bytes=64)
+        nc.sync.dma_start(w4_raw[:].bitcast(I32), w4_words.bitcast(I32).rearrange("a p w -> p a w"))
+        v_sc_rows = keep.tile([P, NP], U8, name="v_sc_rows", align_bytes=64)
+        nc.vector.tensor_copy(v_sc_rows[:], tab_sc[:].indirect(tab_list[:]))
+        v_sc_second = keep.tile([P, NP], U8, name="v_sc_second", align_bytes=64)
+        nc.vector.memset(v_sc_second[96:P, :].bitcast(I32), 0)
+        nc.gpsimd.dma_start(v_sc_second[0 : P - 4, :].bitcast(I32), v_sc_rows[4:P, :].bitcast(I32))
+        v_sc = [v_sc_rows, v_sc_second]
+        load_table(1)
+        nc.sync.dma_start(fresh_list[:], offs2)
+        load_plane(SCATTER_ORDER[0])
+        nc.sync.dma_start(suspect_list[:], offs3)
+        rows = keep.tile([P, P], F32, name="rows")
+        nc.gpsimd.memset(rows[:], 0.0)
+        ident = keep.tile([P, P], F32, name="ident")
+        make_identity(nc, ident[:])
+        for g in range(2):
+            nc.sync.dma_start(
+                rows[4 * g : 4 * g + 4, :].rearrange("t (q r) -> t q r", r=8),
+                gain[512 * g : 512 * (g + 1)].rearrange("(q t r) -> t q r", t=4, r=8),
+            )
+        nc.sync.dma_start(rows[8:10, :], thr.rearrange("(h p) -> h p", h=2))
+
+        def scatter(t):
+            nc.vector.tensor_copy(page[t][:].indirect(fresh_list[:]), fresh[t][:])
+
+        load_plane(SCATTER_ORDER[1])
+
+
+        w1_raw = []
+
+        def load_w1(g):
+            wr = keep.tile([P, 4, 512], F32, name="w1_raw%d" % g, tag="eight", bufs=3, align_bytes=64)
+            nc.sync.dma_start(wr[:], w1[:, 512 * g : 512 * (g + 1)].rearrange("(p j) c -> p j c", j=4))
+            w1_raw.append(wr)
+
+        load_w1(0)
+        load_plane(SCATTER_ORDER[2])
+        load_plane(SCATTER_ORDER[3])
+        load_w1(1)
+        wf_raw = keep.tile([P, 8, N], F32, name="wf_raw", tag="eight", bufs=3, align_bytes=64)
+        wf_rows = wf.rearrange("(g q t r) n -> g t q r n", g=2, t=4, r=8)
+        for s in range(8):
+            nc.sync.dma_start(wf_raw[:, s, :], wf_rows[s // 4, s % 4])
+
+        turned = psum.tile([P, BANK], F32, name="turned", tag="bank")
+        nc.tensor.transpose(turned[:, 0:P], rows[:], ident[:])
+        gain_col = keep.tile([P, 8], F32, name="gain_col")
+        nc.scalar.activation(gain_col[:], turned[:, 0:8], ACT.Copy)
+        minus_thr = keep.tile([P, 2], F32, name="minus_thr")
+        nc.scalar.activation(minus_thr[:], turned[:, 8:10], ACT.Copy, scale=-1.0)
+
+
+        v_w = [keep.tile([P, NP], U32, name="v_w%d" % a, tag="pairs%d" % a, align_bytes=64) for a in range(2)]
+        nc.vector.tensor_copy(v_w[0][:], tab_w[0][:].indirect(tab_list[:]))
+        w4_p = keep.tile([P, 2, 2 * H], U8, name="w4_p", tag="pairs2", align_bytes=64)
+        nc.vector.tensor_copy(
+            w4_p[:].bitcast(I32).rearrange("p a (g t q w) -> p (a g) t q w", g=2, t=4, w=4),
+            w4_raw[:].bitcast(I32).rearrange("p a (g q t w) -> p (a g) t q w", g=2, t=4, w=4),
+        )
+        w4_sc = keep.tile([P, 2, H], U8, name="w4_sc", tag="pairs3", align_bytes=64)
+        nc.vector.tensor_copy(
+            w4_sc[:].bitcast(I32).rearrange("p a (g t q w) -> p (a g) t q w", g=2, t=4, w=2),
+            w4_sc_raw[:].bitcast(I32).rearrange("p a (g q t w) -> p (a g) t q w", g=2, t=4, w=2),
+        )
+        nc.vector.tensor_copy(v_w[1][:], tab_w[1][:].indirect(tab_list[:]))
+        for t in SCATTER_ORDER:
+            scatter(t)
+
+        log_b = [keep.tile([P, 4 * NP], F32, name="log_b%d" % g, align_bytes=64) for g in range(2)]
+
+        def record_tile(s):
+            g, t = divmod(s, 4)
+            for half in range(2):
+                acc = psum.tile([P, BANK], F32, name="acc_b", tag="bank")
+                cols = slice(BANK * half, BANK * (half + 1))
+                for a in range(2):
+                    nc.tensor.matmul_mx(
+                        out=acc[:],
+                        lhsT=w4_p[:, a, 2 * P * s : 2 * P * (s + 1)].bitcast(FP4X4),
+                        lhsT_scale=w4_sc[:, a, P * s : P * (s + 1)],
+                        rhs=v_w[a][:, cols].bitcast(FP8X4),
+                        rhs_scale=v_sc[a][:, cols],
+                        start=(a == 0),
+                        stop=(a == 1),
+                    )
+                first = NP * t + BANK * half
+                nc.scalar.activation(log_b[g][:, first : first + BANK], acc[:], ACT.Square)
+            both = log_b[g][:, NP * t : NP * (t + 1)]
+            nc.scalar.activation(both, both, ACT.Ln, bias=1.0)
+
+        def record_gain(s):
+            g, t = divmod(s, 4)
+            both = log_b[g][:, NP * t : NP * (t + 1)]
+            nc.gpsimd.tensor_scalar(both, both, gain_col[:, s : s + 1], 0.0, ALU.mult, ALU.add)
+
+        for s in range(8):
+            record_tile(s)
+
+        pairs = [
+            keep.tile([P, 4 * BANK], BF16, name="pairs%d" % c, tag="pairs%d" % c, align_bytes=64) for c in range(4)
+        ]
+
+        def cast_plane(t, c):
+            first = 2 * BANK * (t // 2)
+            dst = pairs[c][:, first + t % 2 : first + 2 * BANK : 2]
+            src = page[t][:, BANK * c : BANK * (c + 1)]
+            if t < 2:
+                nc.scalar.copy(dst, src)
+            else:
+                gp_cast(dst, src)
+
+        w1_bf = [keep.tile([P, 4, P, 4], BF16, name="w1_bf%d" % g, align_bytes=64) for g in range(2)]
+        w1_q = keep.tile([P, H], U32, name="w1_q", tag="fresh%d" % SCATTER_ORDER[3], align_bytes=64)
+        w1_sc = keep.tile([P, H], U8, name="w1_sc", align_bytes=64)
+
+        def cast_w1(g):
+            by_tile = w1_raw[g][:].rearrange("p j (q t r i) -> p t q r j i", t=4, r=4, i=2)
+            for t in range(4):
+                nc.scalar.copy(w1_bf[g][:, t, :, :].rearrange("p (q r i) j -> p q r j i", r=4, i=2), by_tile[:, t])
+
+        def quantise_w1(g):
+            cols = slice(512 * g, 512 * (g + 1))
+            nc.vector.quantize_mx(
+                out=w1_q[:, cols].bitcast(FP8X4), scales=w1_sc[:, cols],
+                in_=w1_bf[g][:].rearrange("p t m j -> p (t m j)"),
+            )
+
+        cast_w1(0)
+        for t in SCATTER_ORDER[0:3]:
+            for c in range(4):
+                cast_plane(t, c)
+        cast_w1(1)
+        for s in range(8):
+            record_gain(s)
+        quantise_w1(0)
+
+        page_q = [keep.tile([P, BANK], U32, name="page_q%d" % c, align_bytes=64) for c in range(4)]
+        page_sc = [keep.tile([P, BANK], U8, name="page_sc%d" % c, align_bytes=64) for c in range(4)]
+        for c in range(4):
+            cast_plane(SCATTER_ORDER[3], c)
+        page_bf = []
+        for c in range(5):
+            if c < 4:
+                pb = keep.tile([P, BANK, 4], BF16, name="page_bf", tag="woven", bufs=3, align_bytes=64)
+                nc.vector.tensor_copy(
+                    pb[:].rearrange("p n t -> p (n t)").bitcast(I32).rearrange("p (n i u) -> p n u i", u=2, i=2),
+                    pairs[c][:].bitcast(I32).rearrange("p (u n i) -> p n u i", u=2, i=2),
+                )
+                page_bf.append(pb)
+            if c > 0:
+                nc.vector.quantize_mx(
+                    out=page_q[c - 1][:].bitcast(FP8X4), scales=page_sc[c - 1][:],
+                    in_=page_bf[c - 1][:].rearrange("p n t -> p (n t)"),
+                )
+        quantise_w1(1)
+        wf_bf = keep.tile([P, 2, N, 4], BF16, name="wf_bf", tag="pairs3", align_bytes=64)
+        for g in range(2):
+            gp_cast(wf_bf[:, g, :, :], wf_raw[:, 4 * g : 4 * g + 4, :].rearrange("p t n -> p n t"))
+        wf_q = keep.tile([P, 2 * N], U32, name="wf_q", align_bytes=64)
+        wf_sc = keep.tile([P, 2 * N], U8, name="wf_sc", align_bytes=64)
+
+        log_a = [keep.tile([P, 4 * NP], F32, name="log_a%d" % g, tag="sixteen", bufs=2, align_bytes=64) for g in range(2)]
+        proj = {}
+        h_q = [[keep.tile([P, BANK], U32, name="h_q%d%d" % (g, u), align_bytes=64) for u in range(2)] for g in range(2)]
+        h_sc = [[keep.tile([P, BANK], U8, name="h_sc%d%d" % (g, u), align_bytes=64) for u in range(2)] for g in range(2)]
+        h_bf = {}
+
+        def project(s):
+            proj[s] = keep.tile([P, T2], F32, name="proj", tag="eight", bufs=3, align_bytes=64)
+            for c in range(4):
+                acc = psum.tile([P, BANK], F32, name="acc_a", tag="bank")
+                nc.tensor.matmul_mx(
+                    out=acc[:],
+                    lhsT=w1_q[:, P * s : P * (s + 1)].bitcast(FP8X4),
+                    lhsT_scale=w1_sc[:, P * s : P * (s + 1)],
+                    rhs=page_q[c][:].bitcast(FP8X4),
+                    rhs_scale=page_sc[c][:],
+                    start=True,
+                    stop=True,
+                )
+                if (s, c) in ON_VECTOR:
+                    nc.vector.tensor_copy(proj[s][:, BANK * c : BANK * (c + 1)], acc[:])
+                else:
+                    nc.scalar.copy(proj[s][:, BANK * c : BANK * (c + 1)], acc[:])
+
+        def pieces(s):
+            g, t = divmod(s, 4)
+            if g == 0:
+                return [(log_a[0][:, NP * t : NP * (t + 1)], suspect_list[:])]
+            return [
+                (
+                    log_a[1][:, BANK * (4 * half + t) : BANK * (4 * half + t + 1)],
+                    suspect_list[:, 32 * half : 32 * (half + 1)],
+                )
+                for half in range(2)
+            ]
+
+        def pick(s):
+            for part, offsets in pieces(s):
+                nc.vector.tensor_copy(part, proj[s][:].indirect(offsets))
+
+        def energy(s):
+            for part, offsets in pieces(s):
+                nc.scalar.activation(part, part, ACT.Square)
+                nc.scalar.activation(part, part, ACT.Ln, bias=1.0)
+
+        def weigh(s):
+            for part, offsets in pieces(s):
+                nc.gpsimd.tensor_scalar(part, part, gain_col[:, s : s + 1], 0.0, ALU.mult, ALU.add)
+
+        def compare(g, half):
+            hb = keep.tile([P, BANK, 4], BF16, name="h_bf", tag="woven", bufs=3, align_bytes=64)
+            cols = slice(BANK * half, BANK * (half + 1))
+            if g == 0:
+                suspects = log_a[0][:].rearrange("p (t n) -> p t n", t=4)[:, :, cols]
+            else:
+                suspects = log_a[1][:, 4 * BANK * half : 4 * BANK * (half + 1)].rearrange("p (t n) -> p t n", t=4)
+            records = log_b[g][:].rearrange("p (t n) -> p t n", t=4)[:, :, cols]
+            nc.vector.tensor_tensor(
+                hb[:].rearrange("p (n i) t -> p n t i", i=2),
+                suspects.rearrange("p t (n i) -> p n t i", i=2),
+                records.rearrange("p t (n i) -> p n t i", i=2),
+                ALU.subtract,
+            )
+            h_bf[g, half] = hb
+
+        def quantise_h(g, half):
+            nc.vector.quantize_mx(
+                out=h_q[g][half][:].bitcast(FP8X4), scales=h_sc[g][half][:],
+                in_=h_bf[g, half][:].rearrange("p n t -> p (n t)"),
+            )
+
+        project(0)
+        for s in range(8):
+            if s < 7:
+                project(s + 1)
+            pick(s)
+            if s >= 1:
+                weigh(s - 1)
+            if s == 2:
+                nc.vector.quantize_mx(
+                    out=wf_q[:].bitcast(FP8X4), scales=wf_sc[:], in_=wf_bf[:].rearrange("p g n t -> p (g n t)")
+                )
+            if s == 4:
+                compare(0, 0)
+                compare(0, 1)
+            if s == 5:
+                quantise_h(0, 0)
+                quantise_h(0, 1)
+            energy(s)
+        weigh(7)
+        for half in range(2):
+            compare(1, half)
+        for half in range(2):
+            quantise_h(1, half)
+            cols = slice(BANK * half, BANK * (half + 1))
+            for h in range(2):
+                acc = psum.tile([P, BANK], F32, name="acc_y", tag="bank")
+                for g in range(2):
+                    wcols = slice(N * g + P * h, N * g + P * (h + 1))
+                    nc.tensor.matmul_mx(
+                        out=acc[:],
+                        lhsT=wf_q[:, wcols].bitcast(FP8X4),
+                        lhsT_scale=wf_sc[:, wcols],
+                        rhs=h_q[g][half][:].bitcast(FP8X4),
+                        rhs_scale=h_sc[g][half][:],
+                        start=(g == 0),
+                        stop=(g == 1),
+                    )
+                staged = keep.tile([P, BANK], F32, name="staged%d%d" % (half, h), align_bytes=64)
+                nc.scalar.activation(staged[:], acc[:], ACT.Identity, bias=minus_thr[:, h : h + 1])
+                nc.sync.dma_start(out[P * h : P * (h + 1), cols], staged[:])

@@ -20,7 +20,7 @@ ALU = mybir.AluOpType
 P = 128
 BANK = 512
 SCATTER_ORDER = (0, 2, 3, 1)
-ON_VECTOR = ((0, 3), (1, 3), (2, 3), (3, 3), (4, 3))
+ON_VECTOR = ((0, 3), (1, 3), (2, 3), (3, 3), (4, 3), (5, 3), (6, 3), (7, 2), (7, 3))
 
 
 def tile_list_gnss_spoofing_monitor_kernel(
@@ -57,9 +57,11 @@ def tile_list_gnss_spoofing_monitor_kernel(
         def load_plane(t, pieces=1):
             page[t] = keep.tile([P, T2], F32, name="page%d" % t, align_bytes=64)
             fresh[t] = keep.tile([P, S], F32, name="fresh%d" % t, tag="fresh%d" % t, align_bytes=64)
-            for dst, src, width in ((page[t], base_planes[t], T2 // pieces), (fresh[t], xs_planes[t], S // pieces)):
-                for i in range(pieces):
-                    nc.sync.dma_start(dst[:, width * i : width * (i + 1)], src[:, width * i : width * (i + 1)])
+            nc.sync.dma_start(page[t][:], base_planes[t])
+            width = S // pieces
+            for i in range(pieces):
+                cols = slice(width * i, width * (i + 1))
+                nc.sync.dma_start(fresh[t][:, cols], xs_planes[t][:, cols])
 
         tab_w = []
 
@@ -87,7 +89,7 @@ def tile_list_gnss_spoofing_monitor_kernel(
         v_sc = [v_sc_rows, v_sc_second]
         load_table(1)
         nc.sync.dma_start(fresh_list[:], offs2)
-        load_plane(SCATTER_ORDER[0])
+        load_plane(SCATTER_ORDER[0], pieces=2)
         nc.sync.dma_start(suspect_list[:], offs3)
         rows = keep.tile([P, P], F32, name="rows")
         nc.gpsimd.memset(rows[:], 0.0)
@@ -100,10 +102,11 @@ def tile_list_gnss_spoofing_monitor_kernel(
             )
         nc.sync.dma_start(rows[8:10, :], thr.rearrange("(h p) -> h p", h=2))
 
-        def scatter(t):
-            nc.vector.tensor_copy(page[t][:].indirect(fresh_list[:]), fresh[t][:])
-
-        load_plane(SCATTER_ORDER[1])
+        def scatter(t, pieces):
+            width = S // pieces
+            for i in range(pieces):
+                offsets = fresh_list[:, width // 16 * i : width // 16 * (i + 1)]
+                nc.vector.tensor_copy(page[t][:].indirect(offsets), fresh[t][:, width * i : width * (i + 1)])
 
 
         w1_raw = []
@@ -114,9 +117,10 @@ def tile_list_gnss_spoofing_monitor_kernel(
             w1_raw.append(wr)
 
         load_w1(0)
+        load_plane(SCATTER_ORDER[1])
+        load_w1(1)
         load_plane(SCATTER_ORDER[2])
         load_plane(SCATTER_ORDER[3])
-        load_w1(1)
         wf_raw = keep.tile([P, 8, N], F32, name="wf_raw", tag="eight", bufs=3, align_bytes=64)
         wf_rows = wf.rearrange("(g q t r) n -> g t q r n", g=2, t=4, r=8)
         for s in range(8):
@@ -144,7 +148,7 @@ def tile_list_gnss_spoofing_monitor_kernel(
         )
         nc.vector.tensor_copy(v_w[1][:], tab_w[1][:].indirect(tab_list[:]))
         for t in SCATTER_ORDER:
-            scatter(t)
+            scatter(t, 2 if t == SCATTER_ORDER[0] else 1)
 
         log_b = [keep.tile([P, 4 * NP], F32, name="log_b%d" % g, align_bytes=64) for g in range(2)]
 
@@ -194,9 +198,9 @@ def tile_list_gnss_spoofing_monitor_kernel(
         w1_sc = keep.tile([P, H], U8, name="w1_sc", align_bytes=64)
 
         def cast_w1(g):
-            by_tile = w1_raw[g][:].rearrange("p j (q t r i) -> p t q r j i", t=4, r=4, i=2)
+            by_tile = w1_raw[g][:].rearrange("p j (q t r) -> p t q r j", t=4, r=8)
             for t in range(4):
-                nc.scalar.copy(w1_bf[g][:, t, :, :].rearrange("p (q r i) j -> p q r j i", r=4, i=2), by_tile[:, t])
+                gp_cast(w1_bf[g][:, t, :, :].rearrange("p (q r) j -> p q r j", r=8), by_tile[:, t])
 
         def quantise_w1(g):
             cols = slice(512 * g, 512 * (g + 1))
@@ -206,12 +210,17 @@ def tile_list_gnss_spoofing_monitor_kernel(
             )
 
         cast_w1(0)
+        cast_w1(1)
         for t in SCATTER_ORDER[0:3]:
             for c in range(4):
                 cast_plane(t, c)
-        cast_w1(1)
         for s in range(8):
             record_gain(s)
+        wf_bf = keep.tile([P, 2, N, 4], BF16, name="wf_bf", align_bytes=64)
+        nc.scalar.copy(
+            wf_bf[:].rearrange("p g (n i) t -> p g n t i", i=2),
+            wf_raw[:].rearrange("p (g t) (n i) -> p g n t i", g=2, i=2),
+        )
         quantise_w1(0)
 
         page_q = [keep.tile([P, BANK], U32, name="page_q%d" % c, align_bytes=64) for c in range(4)]
@@ -233,16 +242,16 @@ def tile_list_gnss_spoofing_monitor_kernel(
                     in_=page_bf[c - 1][:].rearrange("p n t -> p (n t)"),
                 )
         quantise_w1(1)
-        wf_bf = keep.tile([P, 2, N, 4], BF16, name="wf_bf", tag="pairs3", align_bytes=64)
-        for g in range(2):
-            gp_cast(wf_bf[:, g, :, :], wf_raw[:, 4 * g : 4 * g + 4, :].rearrange("p t n -> p n t"))
-        wf_q = keep.tile([P, 2 * N], U32, name="wf_q", align_bytes=64)
+        wf_q = keep.tile([P, 2 * N], U32, name="wf_q", tag="pairs3", align_bytes=64)
         wf_sc = keep.tile([P, 2 * N], U8, name="wf_sc", align_bytes=64)
+        nc.vector.quantize_mx(
+            out=wf_q[:].bitcast(FP8X4), scales=wf_sc[:], in_=wf_bf[:].rearrange("p g n t -> p (g n t)")
+        )
 
         log_a = [keep.tile([P, 4 * NP], F32, name="log_a%d" % g, tag="sixteen", bufs=2, align_bytes=64) for g in range(2)]
         proj = {}
-        h_q = [[keep.tile([P, BANK], U32, name="h_q%d%d" % (g, u), align_bytes=64) for u in range(2)] for g in range(2)]
-        h_sc = [[keep.tile([P, BANK], U8, name="h_sc%d%d" % (g, u), align_bytes=64) for u in range(2)] for g in range(2)]
+        h_q = {(1, u): keep.tile([P, BANK], U32, name="h_q1%d" % u, align_bytes=64)[:] for u in range(2)}
+        h_sc = {(1, u): keep.tile([P, BANK], U8, name="h_sc1%d" % u, align_bytes=64)[:] for u in range(2)}
         h_bf = {}
 
         def project(s):
@@ -296,7 +305,8 @@ def tile_list_gnss_spoofing_monitor_kernel(
             else:
                 suspects = log_a[1][:, 4 * BANK * half : 4 * BANK * (half + 1)].rearrange("p (t n) -> p t n", t=4)
             records = log_b[g][:].rearrange("p (t n) -> p t n", t=4)[:, :, cols]
-            nc.vector.tensor_tensor(
+            engine = nc.gpsimd if g == 0 else nc.vector
+            engine.tensor_tensor(
                 hb[:].rearrange("p (n i) t -> p n t i", i=2),
                 suspects.rearrange("p t (n i) -> p n t i", i=2),
                 records.rearrange("p t (n i) -> p n t i", i=2),
@@ -306,7 +316,7 @@ def tile_list_gnss_spoofing_monitor_kernel(
 
         def quantise_h(g, half):
             nc.vector.quantize_mx(
-                out=h_q[g][half][:].bitcast(FP8X4), scales=h_sc[g][half][:],
+                out=h_q[g, half].bitcast(FP8X4), scales=h_sc[g, half],
                 in_=h_bf[g, half][:].rearrange("p n t -> p (n t)"),
             )
 
@@ -317,16 +327,17 @@ def tile_list_gnss_spoofing_monitor_kernel(
             pick(s)
             if s >= 1:
                 weigh(s - 1)
-            if s == 2:
-                nc.vector.quantize_mx(
-                    out=wf_q[:].bitcast(FP8X4), scales=wf_sc[:], in_=wf_bf[:].rearrange("p g n t -> p (g n t)")
-                )
             if s == 4:
                 compare(0, 0)
-                compare(0, 1)
             if s == 5:
-                quantise_h(0, 0)
-                quantise_h(0, 1)
+                compare(0, 1)
+            if s == 7:
+                for half in range(2):
+                    h_sc[0, half] = keep.tile([P, BANK], U8, name="h_sc0", tag="eight", bufs=3, align_bytes=64)[:]
+                first_codes = keep.tile([P, NP], U32, name="h_q0", tag="eight", bufs=3, align_bytes=64)
+                for half in range(2):
+                    h_q[0, half] = first_codes[:, BANK * half : BANK * (half + 1)]
+                    quantise_h(0, half)
             energy(s)
         weigh(7)
         for half in range(2):
@@ -342,8 +353,8 @@ def tile_list_gnss_spoofing_monitor_kernel(
                         out=acc[:],
                         lhsT=wf_q[:, wcols].bitcast(FP8X4),
                         lhsT_scale=wf_sc[:, wcols],
-                        rhs=h_q[g][half][:].bitcast(FP8X4),
-                        rhs_scale=h_sc[g][half][:],
+                        rhs=h_q[g, half].bitcast(FP8X4),
+                        rhs_scale=h_sc[g, half],
                         start=(g == 0),
                         stop=(g == 1),
                     )

@@ -20,7 +20,7 @@ ALU = mybir.AluOpType
 P = 128
 BANK = 512
 SCATTER_ORDER = (0, 2, 3, 1)
-ON_VECTOR = ((0, 3), (1, 3), (2, 3), (3, 3), (4, 3), (5, 3), (6, 3), (7, 2), (7, 3))
+ON_VECTOR = ((0, 3), (1, 3))
 
 
 def tile_list_gnss_spoofing_monitor_kernel(
@@ -251,7 +251,11 @@ def tile_list_gnss_spoofing_monitor_kernel(
         log_a = [keep.tile([P, 4 * NP], F32, name="log_a%d" % g, tag="sixteen", bufs=2, align_bytes=64) for g in range(2)]
         proj = {}
         h_q = {(1, u): keep.tile([P, BANK], U32, name="h_q1%d" % u, align_bytes=64)[:] for u in range(2)}
-        h_sc = {(1, u): keep.tile([P, BANK], U8, name="h_sc1%d" % u, align_bytes=64)[:] for u in range(2)}
+        h_sc = {
+            (g, u): keep.tile([P, BANK], U8, name="h_sc%d%d" % (g, u), align_bytes=64)[:]
+            for g in range(2)
+            for u in range(2)
+        }
         h_bf = {}
 
         def project(s):
@@ -295,18 +299,18 @@ def tile_list_gnss_spoofing_monitor_kernel(
 
         def weigh(s):
             for part, offsets in pieces(s):
-                nc.gpsimd.tensor_scalar(part, part, gain_col[:, s : s + 1], 0.0, ALU.mult, ALU.add)
+                nc.vector.tensor_scalar(part, part, gain_col[:, s : s + 1], None, ALU.mult)
 
         def compare(g, half):
-            hb = keep.tile([P, BANK, 4], BF16, name="h_bf", tag="woven", bufs=3, align_bytes=64)
+            tag = "eight" if g == 0 else "woven"
+            hb = keep.tile([P, BANK, 4], BF16, name="h_bf", tag=tag, bufs=3, align_bytes=64)
             cols = slice(BANK * half, BANK * (half + 1))
             if g == 0:
                 suspects = log_a[0][:].rearrange("p (t n) -> p t n", t=4)[:, :, cols]
             else:
                 suspects = log_a[1][:, 4 * BANK * half : 4 * BANK * (half + 1)].rearrange("p (t n) -> p t n", t=4)
             records = log_b[g][:].rearrange("p (t n) -> p t n", t=4)[:, :, cols]
-            engine = nc.gpsimd if g == 0 else nc.vector
-            engine.tensor_tensor(
+            nc.vector.tensor_tensor(
                 hb[:].rearrange("p (n i) t -> p n t i", i=2),
                 suspects.rearrange("p t (n i) -> p n t i", i=2),
                 records.rearrange("p t (n i) -> p n t i", i=2),
@@ -327,13 +331,10 @@ def tile_list_gnss_spoofing_monitor_kernel(
             pick(s)
             if s >= 1:
                 weigh(s - 1)
-            if s == 4:
+            if s == 6:
                 compare(0, 0)
-            if s == 5:
-                compare(0, 1)
             if s == 7:
-                for half in range(2):
-                    h_sc[0, half] = keep.tile([P, BANK], U8, name="h_sc0", tag="eight", bufs=3, align_bytes=64)[:]
+                compare(0, 1)
                 first_codes = keep.tile([P, NP], U32, name="h_q0", tag="eight", bufs=3, align_bytes=64)
                 for half in range(2):
                     h_q[0, half] = first_codes[:, BANK * half : BANK * (half + 1)]

@@ -20,7 +20,7 @@ ALU = mybir.AluOpType
 P = 128
 BANK = 512
 SCATTER_ORDER = (0, 2, 3, 1)
-ON_VECTOR = ((0, 3), (1, 3))
+ON_VECTOR = ((0, 3), (1, 3), (2, 3), (3, 3), (4, 3))
 
 
 def tile_list_gnss_spoofing_monitor_kernel(
@@ -55,7 +55,7 @@ def tile_list_gnss_spoofing_monitor_kernel(
         fresh = {}
 
         def load_plane(t, pieces=1):
-            page[t] = keep.tile([P, T2], F32, name="page%d" % t, align_bytes=64)
+            page[t] = keep.tile([P, T2], F32, name="page%d" % t, tag="page%d" % t, align_bytes=64)
             fresh[t] = keep.tile([P, S], F32, name="fresh%d" % t, tag="fresh%d" % t, align_bytes=64)
             nc.sync.dma_start(page[t][:], base_planes[t])
             width = S // pieces
@@ -85,7 +85,7 @@ def tile_list_gnss_spoofing_monitor_kernel(
         nc.vector.tensor_copy(v_sc_rows[:], tab_sc[:].indirect(tab_list[:]))
         v_sc_second = keep.tile([P, NP], U8, name="v_sc_second", align_bytes=64)
         nc.vector.memset(v_sc_second[96:P, :].bitcast(I32), 0)
-        nc.gpsimd.dma_start(v_sc_second[0 : P - 4, :].bitcast(I32), v_sc_rows[4:P, :].bitcast(I32))
+        nc.gpsimd.dma_start(v_sc_second[0:112, :].bitcast(I32), v_sc_rows[4:116, :].bitcast(I32))
         v_sc = [v_sc_rows, v_sc_second]
         load_table(1)
         nc.sync.dma_start(fresh_list[:], offs2)
@@ -250,7 +250,11 @@ def tile_list_gnss_spoofing_monitor_kernel(
 
         log_a = [keep.tile([P, 4 * NP], F32, name="log_a%d" % g, tag="sixteen", bufs=2, align_bytes=64) for g in range(2)]
         proj = {}
-        h_q = {(1, u): keep.tile([P, BANK], U32, name="h_q1%d" % u, align_bytes=64)[:] for u in range(2)}
+        h_q = {
+            (g, u): keep.tile([P, BANK], U32, name="h_q%d%d" % (g, u), align_bytes=64)[:]
+            for g in range(2)
+            for u in range(2)
+        }
         h_sc = {
             (g, u): keep.tile([P, BANK], U8, name="h_sc%d%d" % (g, u), align_bytes=64)[:]
             for g in range(2)
@@ -276,45 +280,50 @@ def tile_list_gnss_spoofing_monitor_kernel(
                 else:
                     nc.scalar.copy(proj[s][:, BANK * c : BANK * (c + 1)], acc[:])
 
+        h_planes = [
+            keep.tile([P, 4 * NP], BF16, name="h_planes%d" % g, tag="page%d" % SCATTER_ORDER[g], align_bytes=64)
+            for g in range(2)
+        ]
+
         def pieces(s):
             g, t = divmod(s, 4)
             if g == 0:
-                return [(log_a[0][:, NP * t : NP * (t + 1)], suspect_list[:])]
+                return [(slice(NP * t, NP * (t + 1)), 0, NP)]
             return [
-                (
-                    log_a[1][:, BANK * (4 * half + t) : BANK * (4 * half + t + 1)],
-                    suspect_list[:, 32 * half : 32 * (half + 1)],
-                )
-                for half in range(2)
+                (slice(BANK * (4 * half + t), BANK * (4 * half + t + 1)), BANK * half, BANK) for half in range(2)
             ]
 
         def pick(s):
-            for part, offsets in pieces(s):
-                nc.vector.tensor_copy(part, proj[s][:].indirect(offsets))
+            for place, first, count in pieces(s):
+                offsets = suspect_list[:, first // 16 : (first + count) // 16]
+                nc.vector.tensor_copy(log_a[s // 4][:, place], proj[s][:].indirect(offsets))
 
         def energy(s):
-            for part, offsets in pieces(s):
+            for place, first, count in pieces(s):
+                part = log_a[s // 4][:, place]
                 nc.scalar.activation(part, part, ACT.Square)
                 nc.scalar.activation(part, part, ACT.Ln, bias=1.0)
 
-        def weigh(s):
-            for part, offsets in pieces(s):
-                nc.vector.tensor_scalar(part, part, gain_col[:, s : s + 1], None, ALU.mult)
-
-        def compare(g, half):
-            tag = "eight" if g == 0 else "woven"
-            hb = keep.tile([P, BANK, 4], BF16, name="h_bf", tag=tag, bufs=3, align_bytes=64)
-            cols = slice(BANK * half, BANK * (half + 1))
-            if g == 0:
-                suspects = log_a[0][:].rearrange("p (t n) -> p t n", t=4)[:, :, cols]
-            else:
-                suspects = log_a[1][:, 4 * BANK * half : 4 * BANK * (half + 1)].rearrange("p (t n) -> p t n", t=4)
-            records = log_b[g][:].rearrange("p (t n) -> p t n", t=4)[:, :, cols]
-            nc.vector.tensor_tensor(
-                hb[:].rearrange("p (n i) t -> p n t i", i=2),
-                suspects.rearrange("p t (n i) -> p n t i", i=2),
-                records.rearrange("p t (n i) -> p n t i", i=2),
+        def compare(s, piece):
+            g, t = divmod(s, 4)
+            place, first, count = piece
+            nc.vector.scalar_tensor_tensor(
+                h_planes[g][:, place],
+                log_a[g][:, place],
+                gain_col[:, s : s + 1],
+                log_b[g][:, NP * t + first : NP * t + first + count],
+                ALU.mult,
                 ALU.subtract,
+            )
+
+        def weave(g, half):
+            hb = keep.tile([P, BANK, 4], BF16, name="h_bf", tag="woven", bufs=3, align_bytes=64)
+            if g == 0:
+                planes = h_planes[0][:].rearrange("p (t n) -> p t n", t=4)[:, :, BANK * half : BANK * (half + 1)]
+            else:
+                planes = h_planes[1][:, 4 * BANK * half : 4 * BANK * (half + 1)].rearrange("p (t n) -> p t n", t=4)
+            nc.vector.tensor_copy(
+                hb[:].rearrange("p (n i) t -> p n t i", i=4), planes.rearrange("p t (n i) -> p n t i", i=4)
             )
             h_bf[g, half] = hb
 
@@ -330,19 +339,18 @@ def tile_list_gnss_spoofing_monitor_kernel(
                 project(s + 1)
             pick(s)
             if s >= 1:
-                weigh(s - 1)
-            if s == 6:
-                compare(0, 0)
-            if s == 7:
-                compare(0, 1)
-                first_codes = keep.tile([P, NP], U32, name="h_q0", tag="eight", bufs=3, align_bytes=64)
-                for half in range(2):
-                    h_q[0, half] = first_codes[:, BANK * half : BANK * (half + 1)]
-                    quantise_h(0, half)
+                for piece in pieces(s - 1):
+                    compare(s - 1, piece)
+            if s == 4:
+                weave(0, 0)
+                weave(0, 1)
+            if s == 5:
+                quantise_h(0, 0)
+                quantise_h(0, 1)
             energy(s)
-        weigh(7)
         for half in range(2):
-            compare(1, half)
+            compare(7, pieces(7)[half])
+            weave(1, half)
         for half in range(2):
             quantise_h(1, half)
             cols = slice(BANK * half, BANK * (half + 1))

@@ -20,7 +20,8 @@ ALU = mybir.AluOpType
 P = 128
 BANK = 512
 SCATTER_ORDER = (0, 2, 3, 1)
-ON_VECTOR = ((0, 3), (1, 3), (2, 3), (3, 3), (4, 3))
+FIRST_PIECE = 256
+ON_VECTOR = tuple((s, 3) for s in range(5))
 
 
 def tile_list_gnss_spoofing_monitor_kernel(
@@ -32,128 +33,155 @@ def tile_list_gnss_spoofing_monitor_kernel(
         keep = ctx.enter_context(tc.tile_pool(name="keep", bufs=1))
         psum = ctx.enter_context(tc.psum_pool(name="psum", bufs=8))
 
-        def gp_cast(dst, src):
-            nc.gpsimd.tensor_scalar(dst, src, 1.0, 0.0, ALU.mult, ALU.add)
+        def sbuf(shape, dtype, name, tag=None):
+            return keep.tile(shape, dtype, name=name, tag=tag or name, align_bytes=64)
+
+        def gp_scale(dst, src, factor):
+            nc.gpsimd.tensor_scalar(dst, src, factor, 0.0, ALU.mult, ALU.add)
 
         tab_list = lists.tile([P, NP // 16], U16, name="tab_list")
         fresh_list = lists.tile([P, S // 16], U16, name="fresh_list")
         suspect_list = lists.tile([P, NP // 16], U16, name="suspect_list")
-        tab_sc = keep.tile([P, T], U8, name="tab_sc", align_bytes=64)
+        tab_sc = sbuf([P, T], U8, "tab_sc")
         nc.gpsimd.memset(tab_sc[:].bitcast(I32), 0)
-        w4_sc_raw = keep.tile([P, 2, H], U8, name="w4_sc_raw", align_bytes=64)
+        v_sc_second = sbuf([P, NP], U8, "v_sc_second")
+        nc.vector.memset(v_sc_second[96:P, :].bitcast(I32), 0)
+        w4_sc_raw = sbuf([P, 2, H], U8, "w4_sc_raw")
         nc.vector.memset(w4_sc_raw[:].bitcast(I32), 0)
-        nc.sync.dma_start(tab_list[:], offs)
-        for quad in range(4):
-            nc.sync.dma_start(
-                tab_sc[32 * quad : 32 * quad + 8, :].bitcast(I32),
-                tab_scales[:, 4 * quad : 4 * quad + 4, :].bitcast(I32),
-            )
+        rows = sbuf([P, P], F32, "rows")
+        nc.vector.memset(rows[:], 0.0)
+        ident = sbuf([P, P], F32, "ident")
+        make_identity(nc, ident[:])
 
         base_planes = base.rearrange("(p t) c -> t p c", t=4)
         xs_planes = xs.rearrange("(p t) c -> t p c", t=4)
         page = {}
         fresh = {}
 
-        def load_plane(t, pieces=1):
-            page[t] = keep.tile([P, T2], F32, name="page%d" % t, tag="page%d" % t, align_bytes=64)
-            fresh[t] = keep.tile([P, S], F32, name="fresh%d" % t, tag="fresh%d" % t, align_bytes=64)
-            nc.sync.dma_start(page[t][:], base_planes[t])
-            width = S // pieces
+        def cuts(t):
+            if t == SCATTER_ORDER[0]:
+                return [(FIRST_PIECE * i, FIRST_PIECE * (i + 1)) for i in range(S // FIRST_PIECE)]
+            if t == SCATTER_ORDER[3]:
+                return [(0, S)]
+            return [(0, S // 2), (S // 2, S)]
+
+        def load_plane(t, pieces):
+            page[t] = sbuf([P, T2], F32, "page%d" % t, "page%d" % (t if t > 1 else 0))
+            fresh[t] = sbuf([P, S], F32, "fresh%d" % t)
+            width = T2 // pieces
             for i in range(pieces):
                 cols = slice(width * i, width * (i + 1))
-                nc.sync.dma_start(fresh[t][:, cols], xs_planes[t][:, cols])
+                nc.sync.dma_start(page[t][:, cols], base_planes[t][:, cols])
+            load_fresh(t, 0)
 
-        tab_w = []
+        def load_fresh(t, piece):
+            lo, hi = cuts(t)[piece]
+            nc.sync.dma_start(fresh[t][:, lo:hi], xs_planes[t][:, lo:hi])
+
+        def scatter(t):
+            for lo, hi in cuts(t):
+                nc.vector.tensor_copy(page[t][:].indirect(fresh_list[:, lo // 16 : hi // 16]), fresh[t][:, lo:hi])
+
+        tab_w = [sbuf([P, T], U32, "tab_w%d" % a) for a in range(2)]
 
         def load_table(a):
-            tw = keep.tile([P, T], U32, name="tab_w%d" % a, tag="sixteen", bufs=2, align_bytes=64)
             words = tab_words[a].rearrange("p t i -> p (t i)").bitcast(I32)
-            for half in range(2):
-                cols = slice(T // 2 * half, T // 2 * (half + 1))
-                nc.sync.dma_start(tw[:, cols].bitcast(I32), words[:, cols])
-            tab_w.append(tw)
+            for quad in range(4):
+                if a == 0:
+                    for k in range(2):
+                        nc.sync.dma_start(
+                            tab_sc[32 * quad + 4 * k : 32 * quad + 4 * k + 4, :].bitcast(I32),
+                            tab_scales[k, 4 * quad : 4 * quad + 4, :].bitcast(I32),
+                        )
+                cols = slice(T // 4 * quad, T // 4 * (quad + 1))
+                nc.sync.dma_start(tab_w[a][:, cols].bitcast(I32), words[:, cols])
 
+        w1_raw = []
+
+        def load_w1(g):
+            wr = sbuf([P, 4, 512], F32, "w1_raw%d" % g)
+            nc.sync.dma_start(wr[:], w1[:, 512 * g : 512 * (g + 1)].rearrange("(p j) c -> p j c", j=4))
+            w1_raw.append(wr)
+
+        nc.sync.dma_start(fresh_list[:], offs2)
+        load_plane(SCATTER_ORDER[0], 4)
+        for piece in range(1, S // FIRST_PIECE):
+            load_fresh(SCATTER_ORDER[0], piece)
+        nc.sync.dma_start(tab_list[:], offs)
+        nc.sync.dma_start(suspect_list[:], offs3)
         load_table(0)
+        load_table(1)
+        w4_raw = sbuf([P, 2, 2 * H], U8, "w4_raw")
         for quad in range(4):
             nc.sync.dma_start(
                 w4_sc_raw[32 * quad : 32 * quad + 4, :, :].bitcast(I32),
                 w4_scales[:, 4 * quad : 4 * quad + 4, :].bitcast(I32).rearrange("a r w -> r a w"),
             )
-        w4_raw = keep.tile([P, 2, 2 * H], U8, name="w4_raw", align_bytes=64)
-        nc.sync.dma_start(w4_raw[:].bitcast(I32), w4_words.bitcast(I32).rearrange("a p w -> p a w"))
-        v_sc_rows = keep.tile([P, NP], U8, name="v_sc_rows", align_bytes=64)
-        nc.vector.tensor_copy(v_sc_rows[:], tab_sc[:].indirect(tab_list[:]))
-        v_sc_second = keep.tile([P, NP], U8, name="v_sc_second", align_bytes=64)
-        nc.vector.memset(v_sc_second[96:P, :].bitcast(I32), 0)
-        nc.gpsimd.dma_start(v_sc_second[0:112, :].bitcast(I32), v_sc_rows[4:116, :].bitcast(I32))
-        v_sc = [v_sc_rows, v_sc_second]
-        load_table(1)
-        nc.sync.dma_start(fresh_list[:], offs2)
-        load_plane(SCATTER_ORDER[0], pieces=2)
-        nc.sync.dma_start(suspect_list[:], offs3)
-        rows = keep.tile([P, P], F32, name="rows")
-        nc.gpsimd.memset(rows[:], 0.0)
-        ident = keep.tile([P, P], F32, name="ident")
-        make_identity(nc, ident[:])
+            if quad == 1:
+                nc.sync.dma_start(w4_raw[:].bitcast(I32), w4_words.bitcast(I32).rearrange("a p w -> p a w"))
+        load_plane(SCATTER_ORDER[1], 2)
         for g in range(2):
             nc.sync.dma_start(
                 rows[4 * g : 4 * g + 4, :].rearrange("t (q r) -> t q r", r=8),
                 gain[512 * g : 512 * (g + 1)].rearrange("(q t r) -> t q r", t=4, r=8),
             )
         nc.sync.dma_start(rows[8:10, :], thr.rearrange("(h p) -> h p", h=2))
-
-        def scatter(t, pieces):
-            width = S // pieces
-            for i in range(pieces):
-                offsets = fresh_list[:, width // 16 * i : width // 16 * (i + 1)]
-                nc.vector.tensor_copy(page[t][:].indirect(offsets), fresh[t][:, width * i : width * (i + 1)])
-
-
-        w1_raw = []
-
-        def load_w1(g):
-            wr = keep.tile([P, 4, 512], F32, name="w1_raw%d" % g, tag="eight", bufs=3, align_bytes=64)
-            nc.sync.dma_start(wr[:], w1[:, 512 * g : 512 * (g + 1)].rearrange("(p j) c -> p j c", j=4))
-            w1_raw.append(wr)
-
         load_w1(0)
-        load_plane(SCATTER_ORDER[1])
+        load_fresh(SCATTER_ORDER[1], 1)
+        load_plane(SCATTER_ORDER[2], 1)
         load_w1(1)
-        load_plane(SCATTER_ORDER[2])
-        load_plane(SCATTER_ORDER[3])
-        wf_raw = keep.tile([P, 8, N], F32, name="wf_raw", tag="eight", bufs=3, align_bytes=64)
-        wf_rows = wf.rearrange("(g q t r) n -> g t q r n", g=2, t=4, r=8)
-        for s in range(8):
-            nc.sync.dma_start(wf_raw[:, s, :], wf_rows[s // 4, s % 4])
+        load_fresh(SCATTER_ORDER[2], 1)
 
-        turned = psum.tile([P, BANK], F32, name="turned", tag="bank")
-        nc.tensor.transpose(turned[:, 0:P], rows[:], ident[:])
-        gain_col = keep.tile([P, 8], F32, name="gain_col")
-        nc.scalar.activation(gain_col[:], turned[:, 0:8], ACT.Copy)
-        minus_thr = keep.tile([P, 2], F32, name="minus_thr")
-        nc.scalar.activation(minus_thr[:], turned[:, 8:10], ACT.Copy, scale=-1.0)
+        pairs_tile = sbuf([P, 16 * BANK], BF16, "pairs")
+        pairs = [pairs_tile[:, 4 * BANK * c : 4 * BANK * (c + 1)] for c in range(4)]
 
+        def cast_plane(t):
+            for c in range(4):
+                first = 2 * BANK * (t // 2)
+                dst = pairs[c][:, first + t % 2 : first + 2 * BANK : 2]
+                src = page[t][:, BANK * c : BANK * (c + 1)]
+                if t == SCATTER_ORDER[3]:
+                    nc.scalar.copy(dst, src)
+                else:
+                    gp_scale(dst, src, 1.0)
 
-        v_w = [keep.tile([P, NP], U32, name="v_w%d" % a, tag="pairs%d" % a, align_bytes=64) for a in range(2)]
-        nc.vector.tensor_copy(v_w[0][:], tab_w[0][:].indirect(tab_list[:]))
-        w4_p = keep.tile([P, 2, 2 * H], U8, name="w4_p", tag="pairs2", align_bytes=64)
+        scatter(SCATTER_ORDER[0])
+        cast_plane(SCATTER_ORDER[0])
+        load_plane(SCATTER_ORDER[3], 1)
+        v_sc_rows = sbuf([P, NP], U8, "v_sc_rows")
+        nc.vector.tensor_copy(v_sc_rows[:], tab_sc[:].indirect(tab_list[:]))
+        nc.gpsimd.dma_start(v_sc_second[0:112, :].bitcast(I32), v_sc_rows[4:116, :].bitcast(I32))
+        v_sc = [v_sc_rows, v_sc_second]
+        v_w = [sbuf([P, NP], U32, "v_w%d" % a) for a in range(2)]
+        for a in range(2):
+            nc.vector.tensor_copy(v_w[a][:], tab_w[a][:].indirect(tab_list[:]))
+        w4_p = sbuf([P, 2, 2 * H], U8, "w4_p")
         nc.vector.tensor_copy(
             w4_p[:].bitcast(I32).rearrange("p a (g t q w) -> p (a g) t q w", g=2, t=4, w=4),
             w4_raw[:].bitcast(I32).rearrange("p a (g q t w) -> p (a g) t q w", g=2, t=4, w=4),
         )
-        w4_sc = keep.tile([P, 2, H], U8, name="w4_sc", tag="pairs3", align_bytes=64)
+        w4_sc = sbuf([P, 2, H], U8, "w4_sc")
         nc.vector.tensor_copy(
             w4_sc[:].bitcast(I32).rearrange("p a (g t q w) -> p (a g) t q w", g=2, t=4, w=2),
             w4_sc_raw[:].bitcast(I32).rearrange("p a (g q t w) -> p (a g) t q w", g=2, t=4, w=2),
         )
-        nc.vector.tensor_copy(v_w[1][:], tab_w[1][:].indirect(tab_list[:]))
-        for t in SCATTER_ORDER:
-            scatter(t, 2 if t == SCATTER_ORDER[0] else 1)
+        for t in SCATTER_ORDER[1:]:
+            scatter(t)
 
-        log_b = [keep.tile([P, 4 * NP], F32, name="log_b%d" % g, align_bytes=64) for g in range(2)]
+        turned = psum.tile([P, BANK], F32, name="turned", tag="bank")
+        nc.tensor.transpose(turned[:, 0:P], rows[:], ident[:])
+        gain_col = sbuf([P, 8], F32, "gain_col")
+        nc.scalar.activation(gain_col[:], turned[:, 0:8], ACT.Copy)
+        minus_thr = sbuf([P, 2], F32, "minus_thr")
+        nc.scalar.activation(minus_thr[:], turned[:, 8:10], ACT.Copy, scale=-1.0)
+
+        log_b = [sbuf([P, 4 * NP], F32, "log_b%d" % g) for g in range(2)]
+
+        def plane(tiles, s, lo=0, hi=NP):
+            g, t = divmod(s, 4)
+            return tiles[g][:, NP * t + lo : NP * t + hi]
 
         def record_tile(s):
-            g, t = divmod(s, 4)
             for half in range(2):
                 acc = psum.tile([P, BANK], F32, name="acc_b", tag="bank")
                 cols = slice(BANK * half, BANK * (half + 1))
@@ -167,40 +195,20 @@ def tile_list_gnss_spoofing_monitor_kernel(
                         start=(a == 0),
                         stop=(a == 1),
                     )
-                first = NP * t + BANK * half
-                nc.scalar.activation(log_b[g][:, first : first + BANK], acc[:], ACT.Square)
-            both = log_b[g][:, NP * t : NP * (t + 1)]
-            nc.scalar.activation(both, both, ACT.Ln, bias=1.0)
+                nc.scalar.activation(plane(log_b, s, BANK * half, BANK * (half + 1)), acc[:], ACT.Square)
+            nc.scalar.activation(plane(log_b, s), plane(log_b, s), ACT.Ln, bias=1.0)
 
         def record_gain(s):
-            g, t = divmod(s, 4)
-            both = log_b[g][:, NP * t : NP * (t + 1)]
-            nc.gpsimd.tensor_scalar(both, both, gain_col[:, s : s + 1], 0.0, ALU.mult, ALU.add)
+            gp_scale(plane(gained_b, s), plane(log_b, s), gain_col[:, s : s + 1])
 
-        for s in range(8):
-            record_tile(s)
-
-        pairs = [
-            keep.tile([P, 4 * BANK], BF16, name="pairs%d" % c, tag="pairs%d" % c, align_bytes=64) for c in range(4)
-        ]
-
-        def cast_plane(t, c):
-            first = 2 * BANK * (t // 2)
-            dst = pairs[c][:, first + t % 2 : first + 2 * BANK : 2]
-            src = page[t][:, BANK * c : BANK * (c + 1)]
-            if t < 2:
-                nc.scalar.copy(dst, src)
-            else:
-                gp_cast(dst, src)
-
-        w1_bf = [keep.tile([P, 4, P, 4], BF16, name="w1_bf%d" % g, align_bytes=64) for g in range(2)]
-        w1_q = keep.tile([P, H], U32, name="w1_q", tag="fresh%d" % SCATTER_ORDER[3], align_bytes=64)
-        w1_sc = keep.tile([P, H], U8, name="w1_sc", align_bytes=64)
+        w1_bf = [sbuf([P, 4, P, 4], BF16, "w1_bf%d" % g) for g in range(2)]
+        w1_q = sbuf([P, H], U32, "w1_q", "fresh%d" % SCATTER_ORDER[3])
+        w1_sc = sbuf([P, H], U8, "w1_sc")
 
         def cast_w1(g):
             by_tile = w1_raw[g][:].rearrange("p j (q t r) -> p t q r j", t=4, r=8)
             for t in range(4):
-                gp_cast(w1_bf[g][:, t, :, :].rearrange("p (q r) j -> p q r j", r=8), by_tile[:, t])
+                gp_scale(w1_bf[g][:, t, :, :].rearrange("p (q r) j -> p q r j", r=8), by_tile[:, t], 1.0)
 
         def quantise_w1(g):
             cols = slice(512 * g, 512 * (g + 1))
@@ -209,31 +217,32 @@ def tile_list_gnss_spoofing_monitor_kernel(
                 in_=w1_bf[g][:].rearrange("p t m j -> p (t m j)"),
             )
 
+        gained_b = [log_b[0]]
         cast_w1(0)
-        cast_w1(1)
-        for t in SCATTER_ORDER[0:3]:
-            for c in range(4):
-                cast_plane(t, c)
+        wf_raw = sbuf([P, 8, N], F32, "wf_raw", "w1_raw0")
+        wf_rows = wf.rearrange("(g q t r) n -> g t q r n", g=2, t=4, r=8)
         for s in range(8):
-            record_gain(s)
-        wf_bf = keep.tile([P, 2, N, 4], BF16, name="wf_bf", align_bytes=64)
-        nc.scalar.copy(
-            wf_bf[:].rearrange("p g (n i) t -> p g n t i", i=2),
-            wf_raw[:].rearrange("p (g t) (n i) -> p g n t i", g=2, i=2),
-        )
+            nc.sync.dma_start(wf_raw[:, s, :], wf_rows[s // 4, s % 4])
+        cast_plane(SCATTER_ORDER[1])
+        cast_w1(1)
+        cast_plane(SCATTER_ORDER[2])
+        for s in range(8):
+            if s == 7:
+                cast_plane(SCATTER_ORDER[3])
+            record_tile(s)
+            if s < 4:
+                record_gain(s)
         quantise_w1(0)
 
-        page_q = [keep.tile([P, BANK], U32, name="page_q%d" % c, align_bytes=64) for c in range(4)]
-        page_sc = [keep.tile([P, BANK], U8, name="page_sc%d" % c, align_bytes=64) for c in range(4)]
-        for c in range(4):
-            cast_plane(SCATTER_ORDER[3], c)
+        page_q = [sbuf([P, BANK], U32, "page_q%d" % c) for c in range(4)]
+        page_sc = [sbuf([P, BANK], U8, "page_sc%d" % c) for c in range(4)]
         page_bf = []
         for c in range(5):
             if c < 4:
-                pb = keep.tile([P, BANK, 4], BF16, name="page_bf", tag="woven", bufs=3, align_bytes=64)
+                pb = keep.tile([P, BANK, 4], BF16, name="page_bf", tag="woven", bufs=4, align_bytes=64)
                 nc.vector.tensor_copy(
                     pb[:].rearrange("p n t -> p (n t)").bitcast(I32).rearrange("p (n i u) -> p n u i", u=2, i=2),
-                    pairs[c][:].bitcast(I32).rearrange("p (u n i) -> p n u i", u=2, i=2),
+                    pairs[c].bitcast(I32).rearrange("p (u n i) -> p n u i", u=2, i=2),
                 )
                 page_bf.append(pb)
             if c > 0:
@@ -242,28 +251,24 @@ def tile_list_gnss_spoofing_monitor_kernel(
                     in_=page_bf[c - 1][:].rearrange("p n t -> p (n t)"),
                 )
         quantise_w1(1)
-        wf_q = keep.tile([P, 2 * N], U32, name="wf_q", tag="pairs3", align_bytes=64)
-        wf_sc = keep.tile([P, 2 * N], U8, name="wf_sc", align_bytes=64)
-        nc.vector.quantize_mx(
-            out=wf_q[:].bitcast(FP8X4), scales=wf_sc[:], in_=wf_bf[:].rearrange("p g n t -> p (g n t)")
-        )
+        wf_bf = sbuf([P, 2, N, 4], BF16, "wf_bf", "w1_bf1")
+        for g in range(2):
+            gp_scale(
+                wf_bf[:, g].rearrange("p (n i) t -> p n t i", i=2),
+                wf_raw[:, 4 * g : 4 * g + 4, :].rearrange("p t (n i) -> p n t i", i=2),
+                1.0,
+            )
+        wf_q = sbuf([P, 2 * N], U32, "wf_q", "w4_sc")
+        wf_sc = sbuf([P, 2 * N], U8, "wf_sc")
 
-        log_a = [keep.tile([P, 4 * NP], F32, name="log_a%d" % g, tag="sixteen", bufs=2, align_bytes=64) for g in range(2)]
+        log_a = [sbuf([P, 4 * NP], F32, "log_a%d" % g, "tab_w%d" % g) for g in range(2)]
         proj = {}
-        h_q = {
-            (g, u): keep.tile([P, BANK], U32, name="h_q%d%d" % (g, u), align_bytes=64)[:]
-            for g in range(2)
-            for u in range(2)
-        }
-        h_sc = {
-            (g, u): keep.tile([P, BANK], U8, name="h_sc%d%d" % (g, u), align_bytes=64)[:]
-            for g in range(2)
-            for u in range(2)
-        }
+        h_q = {(g, u): sbuf([P, BANK], U32, "h_q%d%d" % (g, u)) for g in range(2) for u in range(2)}
+        h_sc = {(g, u): sbuf([P, BANK], U8, "h_sc%d%d" % (g, u)) for g in range(2) for u in range(2)}
         h_bf = {}
 
         def project(s):
-            proj[s] = keep.tile([P, T2], F32, name="proj", tag="eight", bufs=3, align_bytes=64)
+            proj[s] = sbuf([P, T2], F32, "proj%d" % s, ("spare", "page2", "page3", "page0")[s % 4])
             for c in range(4):
                 acc = psum.tile([P, BANK], F32, name="acc_a", tag="bank")
                 nc.tensor.matmul_mx(
@@ -280,48 +285,31 @@ def tile_list_gnss_spoofing_monitor_kernel(
                 else:
                     nc.scalar.copy(proj[s][:, BANK * c : BANK * (c + 1)], acc[:])
 
-        h_planes = [
-            keep.tile([P, 4 * NP], BF16, name="h_planes%d" % g, tag="page%d" % SCATTER_ORDER[g], align_bytes=64)
-            for g in range(2)
-        ]
-
         def pieces(s):
-            g, t = divmod(s, 4)
-            if g == 0:
-                return [(slice(NP * t, NP * (t + 1)), 0, NP)]
-            return [
-                (slice(BANK * (4 * half + t), BANK * (4 * half + t + 1)), BANK * half, BANK) for half in range(2)
-            ]
+            return [(0, NP)] if s < 7 else [(0, BANK), (BANK, NP)]
 
         def pick(s):
-            for place, first, count in pieces(s):
-                offsets = suspect_list[:, first // 16 : (first + count) // 16]
-                nc.vector.tensor_copy(log_a[s // 4][:, place], proj[s][:].indirect(offsets))
+            for lo, hi in pieces(s):
+                nc.vector.tensor_copy(plane(log_a, s, lo, hi), proj[s][:].indirect(suspect_list[:, lo // 16 : hi // 16]))
 
         def energy(s):
-            for place, first, count in pieces(s):
-                part = log_a[s // 4][:, place]
+            for lo, hi in pieces(s):
+                part = plane(log_a, s, lo, hi)
                 nc.scalar.activation(part, part, ACT.Square)
                 nc.scalar.activation(part, part, ACT.Ln, bias=1.0)
 
-        def compare(s, piece):
-            g, t = divmod(s, 4)
-            place, first, count = piece
-            nc.vector.scalar_tensor_tensor(
-                h_planes[g][:, place],
-                log_a[g][:, place],
-                gain_col[:, s : s + 1],
-                log_b[g][:, NP * t + first : NP * t + first + count],
-                ALU.mult,
-                ALU.subtract,
-            )
+        h_planes = [sbuf([P, 4 * NP], BF16, "h_planes%d" % g, "w1_raw%d" % g) for g in range(2)]
+
+        def compare(s):
+            for lo, hi in pieces(s):
+                nc.vector.scalar_tensor_tensor(
+                    plane(h_planes, s, lo, hi), plane(log_a, s, lo, hi), gain_col[:, s : s + 1],
+                    plane(gained_b, s, lo, hi), ALU.mult, ALU.subtract,
+                )
 
         def weave(g, half):
-            hb = keep.tile([P, BANK, 4], BF16, name="h_bf", tag="woven", bufs=3, align_bytes=64)
-            if g == 0:
-                planes = h_planes[0][:].rearrange("p (t n) -> p t n", t=4)[:, :, BANK * half : BANK * (half + 1)]
-            else:
-                planes = h_planes[1][:, 4 * BANK * half : 4 * BANK * (half + 1)].rearrange("p (t n) -> p t n", t=4)
+            hb = keep.tile([P, BANK, 4], BF16, name="h_bf", tag="woven", bufs=4, align_bytes=64)
+            planes = h_planes[g][:].rearrange("p (t n) -> p t n", t=4)[:, :, BANK * half : BANK * (half + 1)]
             nc.vector.tensor_copy(
                 hb[:].rearrange("p (n i) t -> p n t i", i=4), planes.rearrange("p t (n i) -> p n t i", i=4)
             )
@@ -329,27 +317,33 @@ def tile_list_gnss_spoofing_monitor_kernel(
 
         def quantise_h(g, half):
             nc.vector.quantize_mx(
-                out=h_q[g, half].bitcast(FP8X4), scales=h_sc[g, half],
+                out=h_q[g, half][:].bitcast(FP8X4), scales=h_sc[g, half][:],
                 in_=h_bf[g, half][:].rearrange("p n t -> p (n t)"),
             )
 
+        gained_b.append(sbuf([P, 4 * NP], F32, "gained_b1", "pairs"))
         project(0)
         for s in range(8):
             if s < 7:
                 project(s + 1)
             pick(s)
+            energy(s)
+            if s < 4:
+                record_gain(4 + s)
+            if s == 1:
+                nc.vector.quantize_mx(
+                    out=wf_q[:].bitcast(FP8X4), scales=wf_sc[:], in_=wf_bf[:].rearrange("p g n t -> p (g n t)")
+                )
             if s >= 1:
-                for piece in pieces(s - 1):
-                    compare(s - 1, piece)
+                compare(s - 1)
             if s == 4:
                 weave(0, 0)
                 weave(0, 1)
             if s == 5:
                 quantise_h(0, 0)
                 quantise_h(0, 1)
-            energy(s)
+        compare(7)
         for half in range(2):
-            compare(7, pieces(7)[half])
             weave(1, half)
         for half in range(2):
             quantise_h(1, half)
@@ -362,11 +356,11 @@ def tile_list_gnss_spoofing_monitor_kernel(
                         out=acc[:],
                         lhsT=wf_q[:, wcols].bitcast(FP8X4),
                         lhsT_scale=wf_sc[:, wcols],
-                        rhs=h_q[g, half].bitcast(FP8X4),
-                        rhs_scale=h_sc[g, half],
+                        rhs=h_q[g, half][:].bitcast(FP8X4),
+                        rhs_scale=h_sc[g, half][:],
                         start=(g == 0),
                         stop=(g == 1),
                     )
-                staged = keep.tile([P, BANK], F32, name="staged%d%d" % (half, h), align_bytes=64)
+                staged = sbuf([P, BANK], F32, "staged%d%d" % (half, h), ("v_w0", "v_w1", "w4_p", "w4_raw")[2 * half + h])
                 nc.scalar.activation(staged[:], acc[:], ACT.Identity, bias=minus_thr[:, h : h + 1])
                 nc.sync.dma_start(out[P * h : P * (h + 1), cols], staged[:])

@@ -1,4 +1,5 @@
 from contextlib import ExitStack
+from itertools import product
 
 import concourse.mybir as mybir
 from concourse.masks import make_identity
@@ -199,10 +200,11 @@ def tile_list_gnss_spoofing_monitor_kernel(
             nc.scalar.activation(plane(log_b, s), plane(log_b, s), ACT.Ln, bias=1.0)
 
         def record_gain(s):
-            gp_scale(plane(gained_b, s), plane(log_b, s), gain_col[:, s : s + 1])
+            gained_b[s] = keep.tile([P, NP], F32, name="gained_b", tag="gained_b", bufs=2, align_bytes=64)
+            gp_scale(gained_b[s][:], plane(log_b, s), gain_col[:, s : s + 1])
 
         w1_bf = [sbuf([P, 4, P, 4], BF16, "w1_bf%d" % g) for g in range(2)]
-        w1_q = sbuf([P, H], U32, "w1_q", "fresh%d" % SCATTER_ORDER[3])
+        w1_q = {}
         w1_sc = sbuf([P, H], U8, "w1_sc")
 
         def cast_w1(g):
@@ -212,12 +214,13 @@ def tile_list_gnss_spoofing_monitor_kernel(
 
         def quantise_w1(g):
             cols = slice(512 * g, 512 * (g + 1))
+            w1_q[g] = sbuf([P, 512], U32, "w1_q%d" % g, ("fresh%d" % SCATTER_ORDER[3], "page_bf2")[g])
             nc.vector.quantize_mx(
-                out=w1_q[:, cols].bitcast(FP8X4), scales=w1_sc[:, cols],
+                out=w1_q[g][:].bitcast(FP8X4), scales=w1_sc[:, cols],
                 in_=w1_bf[g][:].rearrange("p t m j -> p (t m j)"),
             )
 
-        gained_b = [log_b[0]]
+        gained_b = {}
         cast_w1(0)
         wf_raw = sbuf([P, 8, N], F32, "wf_raw", "w1_raw0")
         wf_rows = wf.rearrange("(g q t r) n -> g t q r n", g=2, t=4, r=8)
@@ -230,7 +233,7 @@ def tile_list_gnss_spoofing_monitor_kernel(
             if s == 7:
                 cast_plane(SCATTER_ORDER[3])
             record_tile(s)
-            if s < 4:
+            if s < 2:
                 record_gain(s)
         quantise_w1(0)
 
@@ -239,7 +242,7 @@ def tile_list_gnss_spoofing_monitor_kernel(
         page_bf = []
         for c in range(5):
             if c < 4:
-                pb = keep.tile([P, BANK, 4], BF16, name="page_bf", tag="woven", bufs=4, align_bytes=64)
+                pb = sbuf([P, BANK, 4], BF16, "page_bf%d" % c)
                 nc.vector.tensor_copy(
                     pb[:].rearrange("p n t -> p (n t)").bitcast(I32).rearrange("p (n i u) -> p n u i", u=2, i=2),
                     pairs[c].bitcast(I32).rearrange("p (u n i) -> p n u i", u=2, i=2),
@@ -251,7 +254,7 @@ def tile_list_gnss_spoofing_monitor_kernel(
                     in_=page_bf[c - 1][:].rearrange("p n t -> p (n t)"),
                 )
         quantise_w1(1)
-        wf_bf = sbuf([P, 2, N, 4], BF16, "wf_bf", "w1_bf1")
+        wf_bf = sbuf([P, 2, N, 4], BF16, "wf_bf", "page_bf3")
         for g in range(2):
             gp_scale(
                 wf_bf[:, g].rearrange("p (n i) t -> p n t i", i=2),
@@ -267,13 +270,14 @@ def tile_list_gnss_spoofing_monitor_kernel(
         h_sc = {(g, u): sbuf([P, BANK], U8, "h_sc%d%d" % (g, u)) for g in range(2) for u in range(2)}
         h_bf = {}
 
-        def project(s):
-            proj[s] = sbuf([P, T2], F32, "proj%d" % s, ("spare", "page2", "page3", "page0")[s % 4])
-            for c in range(4):
+        def project(tiles):
+            for s in tiles:
+                proj[s] = sbuf([P, T2], F32, "proj%d" % s, ("spare", "page2", "page3", "page0")[s % 4])
+            for c, s in product(range(4), tiles):
                 acc = psum.tile([P, BANK], F32, name="acc_a", tag="bank")
                 nc.tensor.matmul_mx(
                     out=acc[:],
-                    lhsT=w1_q[:, P * s : P * (s + 1)].bitcast(FP8X4),
+                    lhsT=w1_q[s // 4][:, P * (s % 4) : P * (s % 4 + 1)].bitcast(FP8X4),
                     lhsT_scale=w1_sc[:, P * s : P * (s + 1)],
                     rhs=page_q[c][:].bitcast(FP8X4),
                     rhs_scale=page_sc[c][:],
@@ -304,11 +308,11 @@ def tile_list_gnss_spoofing_monitor_kernel(
             for lo, hi in pieces(s):
                 nc.vector.scalar_tensor_tensor(
                     plane(h_planes, s, lo, hi), plane(log_a, s, lo, hi), gain_col[:, s : s + 1],
-                    plane(gained_b, s, lo, hi), ALU.mult, ALU.subtract,
+                    gained_b[s][:, lo:hi], ALU.mult, ALU.subtract,
                 )
 
         def weave(g, half):
-            hb = keep.tile([P, BANK, 4], BF16, name="h_bf", tag="woven", bufs=4, align_bytes=64)
+            hb = sbuf([P, BANK, 4], BF16, "h_bf%d%d" % (g, half), "page_bf%d" % half)
             planes = h_planes[g][:].rearrange("p (t n) -> p t n", t=4)[:, :, BANK * half : BANK * (half + 1)]
             nc.vector.tensor_copy(
                 hb[:].rearrange("p (n i) t -> p n t i", i=4), planes.rearrange("p t (n i) -> p n t i", i=4)
@@ -321,21 +325,20 @@ def tile_list_gnss_spoofing_monitor_kernel(
                 in_=h_bf[g, half][:].rearrange("p n t -> p (n t)"),
             )
 
-        gained_b.append(sbuf([P, 4 * NP], F32, "gained_b1", "pairs"))
-        project(0)
+        project((0, 1))
         for s in range(8):
-            if s < 7:
-                project(s + 1)
+            if 1 <= s < 7:
+                project((s + 1,))
             pick(s)
             energy(s)
-            if s < 4:
-                record_gain(4 + s)
-            if s == 1:
+            if s == 2:
                 nc.vector.quantize_mx(
                     out=wf_q[:].bitcast(FP8X4), scales=wf_sc[:], in_=wf_bf[:].rearrange("p g n t -> p (g n t)")
                 )
             if s >= 1:
                 compare(s - 1)
+            if 1 <= s < 7:
+                record_gain(s + 1)
             if s == 4:
                 weave(0, 0)
                 weave(0, 1)

@@ -21,8 +21,11 @@ ALU = mybir.AluOpType
 P = 128
 BANK = 512
 SCATTER_ORDER = (0, 2, 3, 1)
-FIRST_PIECE = 256
-ON_VECTOR = tuple((s, 3) for s in range(5))
+END_CHUNKS = ((0, 256), (256, 768), (768, 1024))
+EARLY_GAINS = 5
+QUARTER = 256
+FIRST_PIECE = 512
+ON_VECTOR = tuple((s, 3) for s in range(7))
 
 
 def tile_list_gnss_spoofing_monitor_kernel(
@@ -51,6 +54,16 @@ def tile_list_gnss_spoofing_monitor_kernel(
         nc.vector.memset(w4_sc_raw[:].bitcast(I32), 0)
         rows = sbuf([P, P], F32, "rows")
         nc.vector.memset(rows[:], 0.0)
+        for a, quad in product(range(2), range(4)):
+            nc.gpsimd.dma_start(
+                tab_sc[32 * quad + 4 * a : 32 * quad + 4 * a + 4, :].bitcast(I32),
+                tab_scales[a, 4 * quad : 4 * quad + 4, :].bitcast(I32),
+            )
+        for quad in range(4):
+            nc.gpsimd.dma_start(
+                w4_sc_raw[32 * quad : 32 * quad + 4, :, :].bitcast(I32),
+                w4_scales[:, 4 * quad : 4 * quad + 4, :].bitcast(I32).rearrange("a r w -> r a w"),
+            )
         ident = sbuf([P, P], F32, "ident")
         make_identity(nc, ident[:])
 
@@ -62,12 +75,12 @@ def tile_list_gnss_spoofing_monitor_kernel(
         def cuts(t):
             if t == SCATTER_ORDER[0]:
                 return [(FIRST_PIECE * i, FIRST_PIECE * (i + 1)) for i in range(S // FIRST_PIECE)]
-            if t == SCATTER_ORDER[3]:
-                return [(0, S)]
-            return [(0, S // 2), (S // 2, S)]
+            if t == SCATTER_ORDER[1]:
+                return [(0, S // 2), (S // 2, S)]
+            return [(0, S)]
 
         def load_plane(t, pieces):
-            page[t] = sbuf([P, T2], F32, "page%d" % t, "page%d" % (t if t > 1 else 0))
+            page[t] = sbuf([P, T2], F32, "page%d" % t)
             fresh[t] = sbuf([P, S], F32, "fresh%d" % t)
             width = T2 // pieces
             for i in range(pieces):
@@ -87,14 +100,8 @@ def tile_list_gnss_spoofing_monitor_kernel(
 
         def load_table(a):
             words = tab_words[a].rearrange("p t i -> p (t i)").bitcast(I32)
-            for quad in range(4):
-                if a == 0:
-                    for k in range(2):
-                        nc.sync.dma_start(
-                            tab_sc[32 * quad + 4 * k : 32 * quad + 4 * k + 4, :].bitcast(I32),
-                            tab_scales[k, 4 * quad : 4 * quad + 4, :].bitcast(I32),
-                        )
-                cols = slice(T // 4 * quad, T // 4 * (quad + 1))
+            for half in range(2):
+                cols = slice(T // 2 * half, T // 2 * (half + 1))
                 nc.sync.dma_start(tab_w[a][:, cols].bitcast(I32), words[:, cols])
 
         w1_raw = []
@@ -105,7 +112,7 @@ def tile_list_gnss_spoofing_monitor_kernel(
             w1_raw.append(wr)
 
         nc.sync.dma_start(fresh_list[:], offs2)
-        load_plane(SCATTER_ORDER[0], 4)
+        load_plane(SCATTER_ORDER[0], 1)
         for piece in range(1, S // FIRST_PIECE):
             load_fresh(SCATTER_ORDER[0], piece)
         nc.sync.dma_start(tab_list[:], offs)
@@ -113,14 +120,8 @@ def tile_list_gnss_spoofing_monitor_kernel(
         load_table(0)
         load_table(1)
         w4_raw = sbuf([P, 2, 2 * H], U8, "w4_raw")
-        for quad in range(4):
-            nc.sync.dma_start(
-                w4_sc_raw[32 * quad : 32 * quad + 4, :, :].bitcast(I32),
-                w4_scales[:, 4 * quad : 4 * quad + 4, :].bitcast(I32).rearrange("a r w -> r a w"),
-            )
-            if quad == 1:
-                nc.sync.dma_start(w4_raw[:].bitcast(I32), w4_words.bitcast(I32).rearrange("a p w -> p a w"))
-        load_plane(SCATTER_ORDER[1], 2)
+        nc.sync.dma_start(w4_raw[:].bitcast(I32), w4_words.bitcast(I32).rearrange("a p w -> p a w"))
+        load_plane(SCATTER_ORDER[1], 1)
         for g in range(2):
             nc.sync.dma_start(
                 rows[4 * g : 4 * g + 4, :].rearrange("t (q r) -> t q r", r=8),
@@ -130,8 +131,8 @@ def tile_list_gnss_spoofing_monitor_kernel(
         load_w1(0)
         load_fresh(SCATTER_ORDER[1], 1)
         load_plane(SCATTER_ORDER[2], 1)
+        load_plane(SCATTER_ORDER[3], 1)
         load_w1(1)
-        load_fresh(SCATTER_ORDER[2], 1)
 
         pairs_tile = sbuf([P, 16 * BANK], BF16, "pairs")
         pairs = [pairs_tile[:, 4 * BANK * c : 4 * BANK * (c + 1)] for c in range(4)]
@@ -141,14 +142,13 @@ def tile_list_gnss_spoofing_monitor_kernel(
                 first = 2 * BANK * (t // 2)
                 dst = pairs[c][:, first + t % 2 : first + 2 * BANK : 2]
                 src = page[t][:, BANK * c : BANK * (c + 1)]
-                if t == SCATTER_ORDER[3]:
+                if t < 2:
                     nc.scalar.copy(dst, src)
                 else:
                     gp_scale(dst, src, 1.0)
 
         scatter(SCATTER_ORDER[0])
         cast_plane(SCATTER_ORDER[0])
-        load_plane(SCATTER_ORDER[3], 1)
         v_sc_rows = sbuf([P, NP], U8, "v_sc_rows")
         nc.vector.tensor_copy(v_sc_rows[:], tab_sc[:].indirect(tab_list[:]))
         nc.gpsimd.dma_start(v_sc_second[0:112, :].bitcast(I32), v_sc_rows[4:116, :].bitcast(I32))
@@ -157,12 +157,12 @@ def tile_list_gnss_spoofing_monitor_kernel(
         for a in range(2):
             nc.vector.tensor_copy(v_w[a][:], tab_w[a][:].indirect(tab_list[:]))
         w4_p = sbuf([P, 2, 2 * H], U8, "w4_p")
-        nc.vector.tensor_copy(
+        nc.gpsimd.tensor_copy(
             w4_p[:].bitcast(I32).rearrange("p a (g t q w) -> p (a g) t q w", g=2, t=4, w=4),
             w4_raw[:].bitcast(I32).rearrange("p a (g q t w) -> p (a g) t q w", g=2, t=4, w=4),
         )
         w4_sc = sbuf([P, 2, H], U8, "w4_sc")
-        nc.vector.tensor_copy(
+        nc.gpsimd.tensor_copy(
             w4_sc[:].bitcast(I32).rearrange("p a (g t q w) -> p (a g) t q w", g=2, t=4, w=2),
             w4_sc_raw[:].bitcast(I32).rearrange("p a (g q t w) -> p (a g) t q w", g=2, t=4, w=2),
         )
@@ -200,14 +200,15 @@ def tile_list_gnss_spoofing_monitor_kernel(
             nc.scalar.activation(plane(log_b, s), plane(log_b, s), ACT.Ln, bias=1.0)
 
         def record_gain(s):
-            gained_b[s] = keep.tile([P, NP], F32, name="gained_b", tag="gained_b", bufs=2, align_bytes=64)
-            gp_scale(gained_b[s][:], plane(log_b, s), gain_col[:, s : s + 1])
+            gained_b[s] = plane(log_b, s % EARLY_GAINS)
+            gp_scale(gained_b[s], plane(log_b, s), gain_col[:, s : s + 1])
 
-        w1_bf = [sbuf([P, 4, P, 4], BF16, "w1_bf%d" % g) for g in range(2)]
+        w1_bf = {}
         w1_q = {}
         w1_sc = sbuf([P, H], U8, "w1_sc")
 
         def cast_w1(g):
+            w1_bf[g] = sbuf([P, 4, P, 4], BF16, "w1_bf%d" % g)
             by_tile = w1_raw[g][:].rearrange("p j (q t r) -> p t q r j", t=4, r=8)
             for t in range(4):
                 gp_scale(w1_bf[g][:, t, :, :].rearrange("p (q r) j -> p q r j", r=8), by_tile[:, t], 1.0)
@@ -227,13 +228,12 @@ def tile_list_gnss_spoofing_monitor_kernel(
         for s in range(8):
             nc.sync.dma_start(wf_raw[:, s, :], wf_rows[s // 4, s % 4])
         cast_plane(SCATTER_ORDER[1])
-        cast_w1(1)
         cast_plane(SCATTER_ORDER[2])
         for s in range(8):
             if s == 7:
                 cast_plane(SCATTER_ORDER[3])
             record_tile(s)
-            if s < 2:
+            if s < EARLY_GAINS:
                 record_gain(s)
         quantise_w1(0)
 
@@ -253,26 +253,27 @@ def tile_list_gnss_spoofing_monitor_kernel(
                     out=page_q[c - 1][:].bitcast(FP8X4), scales=page_sc[c - 1][:],
                     in_=page_bf[c - 1][:].rearrange("p n t -> p (n t)"),
                 )
+        w1_bf[1] = sbuf([P, 4, P, 4], BF16, "w1_bf1", "page_bf3")
+        nc.vector.tensor_copy(
+            w1_bf[1][:].rearrange("p t (q r) j -> p t q r j", r=8),
+            w1_raw[1][:].rearrange("p j (q t r) -> p t q r j", t=4, r=8),
+        )
         quantise_w1(1)
         wf_bf = sbuf([P, 2, N, 4], BF16, "wf_bf", "page_bf3")
         for g in range(2):
-            gp_scale(
-                wf_bf[:, g].rearrange("p (n i) t -> p n t i", i=2),
-                wf_raw[:, 4 * g : 4 * g + 4, :].rearrange("p t (n i) -> p n t i", i=2),
-                1.0,
-            )
+            gp_scale(wf_bf[:, g], wf_raw[:, 4 * g : 4 * g + 4, :].rearrange("p t n -> p n t"), 1.0)
         wf_q = sbuf([P, 2 * N], U32, "wf_q", "w4_sc")
         wf_sc = sbuf([P, 2 * N], U8, "wf_sc")
 
         log_a = [sbuf([P, 4 * NP], F32, "log_a%d" % g, "tab_w%d" % g) for g in range(2)]
         proj = {}
-        h_q = {(g, u): sbuf([P, BANK], U32, "h_q%d%d" % (g, u)) for g in range(2) for u in range(2)}
-        h_sc = {(g, u): sbuf([P, BANK], U8, "h_sc%d%d" % (g, u)) for g in range(2) for u in range(2)}
+        h_q = {1: sbuf([P, NP], U32, "h_q1")}
+        h_sc = [sbuf([P, NP], U8, "h_sc%d" % g) for g in range(2)]
         h_bf = {}
 
         def project(tiles):
             for s in tiles:
-                proj[s] = sbuf([P, T2], F32, "proj%d" % s, ("spare", "page2", "page3", "page0")[s % 4])
+                proj[s] = sbuf([P, T2], F32, "proj%d" % s, ("page0", "page2", "page3", "page1")[s % 4])
             for c, s in product(range(4), tiles):
                 acc = psum.tile([P, BANK], F32, name="acc_a", tag="bank")
                 nc.tensor.matmul_mx(
@@ -289,81 +290,106 @@ def tile_list_gnss_spoofing_monitor_kernel(
                 else:
                     nc.scalar.copy(proj[s][:, BANK * c : BANK * (c + 1)], acc[:])
 
-        def pieces(s):
-            return [(0, NP)] if s < 7 else [(0, BANK), (BANK, NP)]
+        def pick(s, lo, hi):
+            nc.vector.tensor_copy(plane(log_a, s, lo, hi), proj[s][:].indirect(suspect_list[:, lo // 16 : hi // 16]))
 
-        def pick(s):
-            for lo, hi in pieces(s):
-                nc.vector.tensor_copy(plane(log_a, s, lo, hi), proj[s][:].indirect(suspect_list[:, lo // 16 : hi // 16]))
+        def energy(s, lo, hi):
+            part = plane(log_a, s, lo, hi)
+            nc.scalar.activation(part, part, ACT.Square)
+            nc.scalar.activation(part, part, ACT.Ln, bias=1.0)
 
-        def energy(s):
-            for lo, hi in pieces(s):
-                part = plane(log_a, s, lo, hi)
-                nc.scalar.activation(part, part, ACT.Square)
-                nc.scalar.activation(part, part, ACT.Ln, bias=1.0)
+        h_planes = [sbuf([P, 4 * NP], BF16, "h_planes%d" % g, ("pairs", "w1_raw1")[g]) for g in range(2)]
 
-        h_planes = [sbuf([P, 4 * NP], BF16, "h_planes%d" % g, "w1_raw%d" % g) for g in range(2)]
+        def compare(s, lo, hi):
+            nc.vector.scalar_tensor_tensor(
+                plane(h_planes, s, lo, hi), plane(log_a, s, lo, hi), gain_col[:, s : s + 1],
+                gained_b[s][:, lo:hi], ALU.mult, ALU.subtract,
+            )
 
-        def compare(s):
-            for lo, hi in pieces(s):
-                nc.vector.scalar_tensor_tensor(
-                    plane(h_planes, s, lo, hi), plane(log_a, s, lo, hi), gain_col[:, s : s + 1],
-                    gained_b[s][:, lo:hi], ALU.mult, ALU.subtract,
+        def weave(copy, g, lo, hi, parts=1, run=4, woven=None):
+            if woven is None:
+                woven = sbuf([P, 4 * (hi - lo)], BF16, "h_bf%d_%d" % (g, lo))[:]
+            h_bf[g, lo] = woven
+            width = (hi - lo) // parts
+            for k in range(parts):
+                planes = h_planes[g][:].rearrange("p (t n) -> p t n", t=4)[:, :, lo + width * k : lo + width * (k + 1)]
+                copy(
+                    woven[:, 4 * width * k : 4 * width * (k + 1)].rearrange("p (n i t) -> p n t i", i=run, t=4),
+                    planes.rearrange("p t (n i) -> p n t i", i=run),
                 )
 
-        def weave(g, half):
-            hb = sbuf([P, BANK, 4], BF16, "h_bf%d%d" % (g, half), "page_bf%d" % half)
-            planes = h_planes[g][:].rearrange("p (t n) -> p t n", t=4)[:, :, BANK * half : BANK * (half + 1)]
-            nc.vector.tensor_copy(
-                hb[:].rearrange("p (n i) t -> p n t i", i=4), planes.rearrange("p t (n i) -> p n t i", i=4)
-            )
-            h_bf[g, half] = hb
-
-        def quantise_h(g, half):
+        def quantise_h(g, lo, hi):
             nc.vector.quantize_mx(
-                out=h_q[g, half][:].bitcast(FP8X4), scales=h_sc[g, half][:],
-                in_=h_bf[g, half][:].rearrange("p n t -> p (n t)"),
+                out=h_q[g][:, lo:hi].bitcast(FP8X4), scales=h_sc[g][:, lo:hi], in_=h_bf[g, lo]
             )
+
+        acc_y = {}
+
+        def alarm_pass(g, lo, hi):
+            for h in range(2):
+                if g == 0:
+                    acc_y[lo, h] = psum.tile([P, BANK], F32, name="acc_y", tag="bank")
+                wcols = slice(N * g + P * h, N * g + P * (h + 1))
+                nc.tensor.matmul_mx(
+                    out=acc_y[lo, h][:, 0 : hi - lo],
+                    lhsT=wf_q[:, wcols].bitcast(FP8X4),
+                    lhsT_scale=wf_sc[:, wcols],
+                    rhs=h_q[g][:, lo:hi].bitcast(FP8X4),
+                    rhs_scale=h_sc[g][:, lo:hi],
+                    start=(g == 0),
+                    stop=(g == 1),
+                )
+
+        def store(lo, hi):
+            for h in range(2):
+                acc = acc_y[lo, h][:, 0 : hi - lo]
+                staged = staged_tile[:, NP * h + lo : NP * h + hi]
+                if h == 1 and hi == NP:
+                    nc.vector.tensor_scalar_add(staged, acc, minus_thr[:, h : h + 1])
+                else:
+                    nc.scalar.activation(staged, acc, ACT.Identity, bias=minus_thr[:, h : h + 1])
+                nc.sync.dma_start(out[P * h : P * (h + 1), lo:hi], staged)
 
         project((0, 1))
-        for s in range(8):
-            if 1 <= s < 7:
+        for s in range(7):
+            if s >= 1:
                 project((s + 1,))
-            pick(s)
-            energy(s)
+            pick(s, 0, NP)
+            energy(s, 0, NP)
             if s == 2:
                 nc.vector.quantize_mx(
                     out=wf_q[:].bitcast(FP8X4), scales=wf_sc[:], in_=wf_bf[:].rearrange("p g n t -> p (g n t)")
                 )
-            if s >= 1:
-                compare(s - 1)
-            if 1 <= s < 7:
-                record_gain(s + 1)
-            if s == 4:
-                weave(0, 0)
-                weave(0, 1)
             if s == 5:
-                quantise_h(0, 0)
-                quantise_h(0, 1)
-        compare(7)
-        for half in range(2):
-            weave(1, half)
-        for half in range(2):
-            quantise_h(1, half)
-            cols = slice(BANK * half, BANK * (half + 1))
-            for h in range(2):
-                acc = psum.tile([P, BANK], F32, name="acc_y", tag="bank")
-                for g in range(2):
-                    wcols = slice(N * g + P * h, N * g + P * (h + 1))
-                    nc.tensor.matmul_mx(
-                        out=acc[:],
-                        lhsT=wf_q[:, wcols].bitcast(FP8X4),
-                        lhsT_scale=wf_sc[:, wcols],
-                        rhs=h_q[g, half][:].bitcast(FP8X4),
-                        rhs_scale=h_sc[g, half][:],
-                        start=(g == 0),
-                        stop=(g == 1),
-                    )
-                staged = sbuf([P, BANK], F32, "staged%d%d" % (half, h), ("v_w0", "v_w1", "w4_p", "w4_raw")[2 * half + h])
-                nc.scalar.activation(staged[:], acc[:], ACT.Identity, bias=minus_thr[:, h : h + 1])
-                nc.sync.dma_start(out[P * h : P * (h + 1), cols], staged[:])
+                weave(nc.vector.tensor_copy, 0, 0, QUARTER, woven=sbuf([P, NP], BF16, "h_bf_first", "page2")[:])
+            if s == 6:
+                h_q[0] = sbuf([P, NP], U32, "h_q0", "page3")
+                for k in (0, 1):
+                    quantise_h(0, QUARTER * k, QUARTER * (k + 1))
+            if s >= 1:
+                compare(s - 1, 0, NP)
+            if s >= 4:
+                lo = QUARTER * (s - 3)
+                released = gained_b[s - 1][:, 0 : NP // 2].bitcast(BF16)
+                weave(lambda dst, src: gp_scale(dst, src, 1.0), 0, lo, lo + QUARTER, 1, 1, released)
+            if 1 <= s <= 8 - EARLY_GAINS:
+                record_gain(EARLY_GAINS + s - 1)
+        staged_tile = sbuf([P, 2 * NP], F32, "staged", "w1_raw0")
+        first, second, last = END_CHUNKS
+        for chunk in END_CHUNKS:
+            pick(7, *chunk)
+            energy(7, *chunk)
+        compare(6, 0, NP)
+        for chunk in END_CHUNKS:
+            compare(7, *chunk)
+        weave(nc.scalar.copy, 1, *first)
+        for k in (2, 3):
+            quantise_h(0, QUARTER * k, QUARTER * (k + 1))
+        for chunk in END_CHUNKS:
+            alarm_pass(0, *chunk)
+        weave(nc.vector.tensor_copy, 1, *second)
+        weave(nc.vector.tensor_copy, 1, *last)
+        for chunk in END_CHUNKS:
+            quantise_h(1, *chunk)
+            alarm_pass(1, *chunk)
+            store(*chunk)

@@ -24,8 +24,10 @@ SCATTER_ORDER = (0, 2, 3, 1)
 END_CHUNKS = ((0, 256), (256, 768), (768, 1024))
 EARLY_GAINS = 5
 QUARTER = 256
+ROW0 = 22
+STAGED_TILES = 2
 FIRST_PIECE = 512
-ON_VECTOR = tuple((s, 3) for s in range(7))
+ON_VECTOR = tuple((s, 3) for s in range(6))
 
 
 def tile_list_gnss_spoofing_monitor_kernel(
@@ -47,23 +49,18 @@ def tile_list_gnss_spoofing_monitor_kernel(
         fresh_list = lists.tile([P, S // 16], U16, name="fresh_list")
         suspect_list = lists.tile([P, NP // 16], U16, name="suspect_list")
         tab_sc = sbuf([P, T], U8, "tab_sc")
-        nc.gpsimd.memset(tab_sc[:].bitcast(I32), 0)
-        v_sc_second = sbuf([P, NP], U8, "v_sc_second")
-        nc.vector.memset(v_sc_second[96:P, :].bitcast(I32), 0)
-        w4_sc_raw = sbuf([P, 2, H], U8, "w4_sc_raw")
-        nc.vector.memset(w4_sc_raw[:].bitcast(I32), 0)
-        rows = sbuf([P, P], F32, "rows")
-        nc.vector.memset(rows[:], 0.0)
-        for a, quad in product(range(2), range(4)):
-            nc.gpsimd.dma_start(
-                tab_sc[32 * quad + 4 * a : 32 * quad + 4 * a + 4, :].bitcast(I32),
-                tab_scales[a, 4 * quad : 4 * quad + 4, :].bitcast(I32),
-            )
         for quad in range(4):
-            nc.gpsimd.dma_start(
-                w4_sc_raw[32 * quad : 32 * quad + 4, :, :].bitcast(I32),
-                w4_scales[:, 4 * quad : 4 * quad + 4, :].bitcast(I32).rearrange("a r w -> r a w"),
-            )
+            engine = nc.gpsimd if quad < 3 else nc.vector
+            engine.memset(tab_sc[32 * quad : 32 * quad + 24, :].bitcast(I32), 0)
+        v_sc = [sbuf([P, NP], U8, "v_sc%d" % a) for a in range(2)]
+        for a in range(2):
+            nc.vector.memset(v_sc[a][96:P, :].bitcast(I32), 0)
+        w4_sc_raw = sbuf([P, 2, H], U8, "w4_sc_raw")
+        w4_sc = sbuf([P, 2, H], U8, "w4_sc")
+        nc.vector.memset(w4_sc[:].bitcast(I32), 0)
+        rows = sbuf([P, P], F32, "rows")
+        for lo, hi in ((0, ROW0), (32, 64), (64, P)):
+            nc.vector.memset(rows[lo:hi, :], 0.0)
         ident = sbuf([P, P], F32, "ident")
         make_identity(nc, ident[:])
 
@@ -75,8 +72,8 @@ def tile_list_gnss_spoofing_monitor_kernel(
         def cuts(t):
             if t == SCATTER_ORDER[0]:
                 return [(FIRST_PIECE * i, FIRST_PIECE * (i + 1)) for i in range(S // FIRST_PIECE)]
-            if t == SCATTER_ORDER[1]:
-                return [(0, S // 2), (S // 2, S)]
+            if t != SCATTER_ORDER[3]:
+                return [(0, S // 4), (S // 4, S)]
             return [(0, S)]
 
         def load_plane(t, pieces):
@@ -98,11 +95,10 @@ def tile_list_gnss_spoofing_monitor_kernel(
 
         tab_w = [sbuf([P, T], U32, "tab_w%d" % a) for a in range(2)]
 
-        def load_table(a):
+        def load_table(a, half):
             words = tab_words[a].rearrange("p t i -> p (t i)").bitcast(I32)
-            for half in range(2):
-                cols = slice(T // 2 * half, T // 2 * (half + 1))
-                nc.sync.dma_start(tab_w[a][:, cols].bitcast(I32), words[:, cols])
+            cols = slice(T // 2 * half, T // 2 * (half + 1))
+            nc.sync.dma_start(tab_w[a][:, cols].bitcast(I32), words[:, cols])
 
         w1_raw = []
 
@@ -111,27 +107,45 @@ def tile_list_gnss_spoofing_monitor_kernel(
             nc.sync.dma_start(wr[:], w1[:, 512 * g : 512 * (g + 1)].rearrange("(p j) c -> p j c", j=4))
             w1_raw.append(wr)
 
+        nc.sync.dma_start(tab_list[:], offs)
+        for quad in range(4):
+            nc.sync.dma_start(
+                tab_sc[32 * quad + 24 : 32 * quad + 32, :].bitcast(I32),
+                tab_scales[:, 4 * quad : 4 * quad + 4, :].bitcast(I32),
+            )
         nc.sync.dma_start(fresh_list[:], offs2)
         load_plane(SCATTER_ORDER[0], 1)
         for piece in range(1, S // FIRST_PIECE):
             load_fresh(SCATTER_ORDER[0], piece)
-        nc.sync.dma_start(tab_list[:], offs)
-        nc.sync.dma_start(suspect_list[:], offs3)
-        load_table(0)
-        load_table(1)
-        w4_raw = sbuf([P, 2, 2 * H], U8, "w4_raw")
-        nc.sync.dma_start(w4_raw[:].bitcast(I32), w4_words.bitcast(I32).rearrange("a p w -> p a w"))
-        load_plane(SCATTER_ORDER[1], 1)
-        for g in range(2):
-            nc.sync.dma_start(
-                rows[4 * g : 4 * g + 4, :].rearrange("t (q r) -> t q r", r=8),
+        small_loads = [
+            (
+                w4_sc_raw[32 * quad : 32 * quad + 4, :, :].bitcast(I32),
+                w4_scales[:, 4 * quad : 4 * quad + 4, :].bitcast(I32).rearrange("a r w -> r a w"),
+            )
+            for quad in range(4)
+        ]
+        small_loads += [
+            (
+                rows[ROW0 + 4 * g : ROW0 + 4 * g + 4, :].rearrange("t (q r) -> t q r", r=8),
                 gain[512 * g : 512 * (g + 1)].rearrange("(q t r) -> t q r", t=4, r=8),
             )
-        nc.sync.dma_start(rows[8:10, :], thr.rearrange("(h p) -> h p", h=2))
-        load_w1(0)
+            for g in range(2)
+        ]
+        small_loads += [(rows[ROW0 + 8 : ROW0 + 10, :], thr.rearrange("(h p) -> h p", h=2))]
+        w4_raw = sbuf([P, 2, 2 * H], U8, "w4_raw")
+        for k in range(4):
+            for dst, src in small_loads[2 * k : 2 * k + 2]:
+                nc.sync.dma_start(dst, src)
+            if k == 2:
+                nc.sync.dma_start(w4_raw[:].bitcast(I32), w4_words.bitcast(I32).rearrange("a p w -> p a w"))
+            load_table(*divmod(k, 2))
+        load_plane(SCATTER_ORDER[1], 1)
         load_fresh(SCATTER_ORDER[1], 1)
         load_plane(SCATTER_ORDER[2], 1)
+        load_w1(0)
+        load_fresh(SCATTER_ORDER[2], 1)
         load_plane(SCATTER_ORDER[3], 1)
+        nc.sync.dma_start(suspect_list[:], offs3)
         load_w1(1)
 
         pairs_tile = sbuf([P, 16 * BANK], BF16, "pairs")
@@ -147,24 +161,26 @@ def tile_list_gnss_spoofing_monitor_kernel(
                 else:
                     gp_scale(dst, src, 1.0)
 
-        scatter(SCATTER_ORDER[0])
-        cast_plane(SCATTER_ORDER[0])
         v_sc_rows = sbuf([P, NP], U8, "v_sc_rows")
         nc.vector.tensor_copy(v_sc_rows[:], tab_sc[:].indirect(tab_list[:]))
-        nc.gpsimd.dma_start(v_sc_second[0:112, :].bitcast(I32), v_sc_rows[4:116, :].bitcast(I32))
-        v_sc = [v_sc_rows, v_sc_second]
+        for a in range(2):
+            first_row = 24 + 4 * a
+            nc.gpsimd.dma_start(v_sc[a][0 : P - first_row, :].bitcast(I32), v_sc_rows[first_row:P, :].bitcast(I32))
+        scatter(SCATTER_ORDER[0])
+        cast_plane(SCATTER_ORDER[0])
         v_w = [sbuf([P, NP], U32, "v_w%d" % a) for a in range(2)]
         for a in range(2):
             nc.vector.tensor_copy(v_w[a][:], tab_w[a][:].indirect(tab_list[:]))
         w4_p = sbuf([P, 2, 2 * H], U8, "w4_p")
+        for quad in range(4):
+            live = slice(32 * quad, 32 * quad + 4)
+            nc.gpsimd.tensor_copy(
+                w4_sc[live].bitcast(I32).rearrange("p a (g t q w) -> p (a g) t q w", g=2, t=4, w=2),
+                w4_sc_raw[live].bitcast(I32).rearrange("p a (g q t w) -> p (a g) t q w", g=2, t=4, w=2),
+            )
         nc.gpsimd.tensor_copy(
             w4_p[:].bitcast(I32).rearrange("p a (g t q w) -> p (a g) t q w", g=2, t=4, w=4),
             w4_raw[:].bitcast(I32).rearrange("p a (g q t w) -> p (a g) t q w", g=2, t=4, w=4),
-        )
-        w4_sc = sbuf([P, 2, H], U8, "w4_sc")
-        nc.gpsimd.tensor_copy(
-            w4_sc[:].bitcast(I32).rearrange("p a (g t q w) -> p (a g) t q w", g=2, t=4, w=2),
-            w4_sc_raw[:].bitcast(I32).rearrange("p a (g q t w) -> p (a g) t q w", g=2, t=4, w=2),
         )
         for t in SCATTER_ORDER[1:]:
             scatter(t)
@@ -172,9 +188,9 @@ def tile_list_gnss_spoofing_monitor_kernel(
         turned = psum.tile([P, BANK], F32, name="turned", tag="bank")
         nc.tensor.transpose(turned[:, 0:P], rows[:], ident[:])
         gain_col = sbuf([P, 8], F32, "gain_col")
-        nc.scalar.activation(gain_col[:], turned[:, 0:8], ACT.Copy)
+        nc.scalar.activation(gain_col[:], turned[:, ROW0 : ROW0 + 8], ACT.Copy)
         minus_thr = sbuf([P, 2], F32, "minus_thr")
-        nc.scalar.activation(minus_thr[:], turned[:, 8:10], ACT.Copy, scale=-1.0)
+        nc.scalar.activation(minus_thr[:], turned[:, ROW0 + 8 : ROW0 + 10], ACT.Copy, scale=-1.0)
 
         log_b = [sbuf([P, 4 * NP], F32, "log_b%d" % g) for g in range(2)]
 
@@ -197,11 +213,20 @@ def tile_list_gnss_spoofing_monitor_kernel(
                         stop=(a == 1),
                     )
                 nc.scalar.activation(plane(log_b, s, BANK * half, BANK * (half + 1)), acc[:], ACT.Square)
-            nc.scalar.activation(plane(log_b, s), plane(log_b, s), ACT.Ln, bias=1.0)
+            nc.scalar.activation(by_halves(logs(s)), by_halves(plane(log_b, s)), ACT.Ln, bias=1.0)
 
-        def record_gain(s):
-            gained_b[s] = plane(log_b, s % EARLY_GAINS)
-            gp_scale(gained_b[s], plane(log_b, s), gain_col[:, s : s + 1])
+        def by_halves(values):
+            return values if values.ndim == 3 else values.rearrange("p (u n) -> p u n", u=2)
+
+        def logs(s):
+            if s >= STAGED_TILES:
+                return plane(log_b, s)
+            words = pairs_tile[:].bitcast(F32).rearrange("p (c half n) -> p c half n", c=4, half=2)
+            return words[:, 2 * s : 2 * s + 2, 1, :]
+
+        def record_gain(s, dst=None):
+            gained_b[s] = plane(log_b, s % EARLY_GAINS) if dst is None else dst
+            gp_scale(by_halves(gained_b[s]), by_halves(logs(s)), gain_col[:, s : s + 1])
 
         w1_bf = {}
         w1_q = {}
@@ -222,19 +247,20 @@ def tile_list_gnss_spoofing_monitor_kernel(
             )
 
         gained_b = {}
-        cast_w1(0)
-        wf_raw = sbuf([P, 8, N], F32, "wf_raw", "w1_raw0")
         wf_rows = wf.rearrange("(g q t r) n -> g t q r n", g=2, t=4, r=8)
-        for s in range(8):
-            nc.sync.dma_start(wf_raw[:, s, :], wf_rows[s // 4, s % 4])
-        cast_plane(SCATTER_ORDER[1])
-        cast_plane(SCATTER_ORDER[2])
         for s in range(8):
             if s == 7:
                 cast_plane(SCATTER_ORDER[3])
             record_tile(s)
-            if s < EARLY_GAINS:
+            if s < EARLY_GAINS - 1:
                 record_gain(s)
+            if s == STAGED_TILES - 1:
+                cast_plane(SCATTER_ORDER[1])
+                cast_w1(0)
+                wf_raw = sbuf([P, 8, N], F32, "wf_raw", "w1_raw0")
+                for k in range(8):
+                    nc.sync.dma_start(wf_raw[:, k, :], wf_rows[k // 4, k % 4])
+                cast_plane(SCATTER_ORDER[2])
         quantise_w1(0)
 
         page_q = [sbuf([P, BANK], U32, "page_q%d" % c) for c in range(4)]
@@ -259,7 +285,9 @@ def tile_list_gnss_spoofing_monitor_kernel(
             w1_raw[1][:].rearrange("p j (q t r) -> p t q r j", t=4, r=8),
         )
         quantise_w1(1)
-        wf_bf = sbuf([P, 2, N, 4], BF16, "wf_bf", "page_bf3")
+        late = sbuf([P, 2 * NP], F32, "late", "page_bf3")
+        record_gain(EARLY_GAINS - 1, late[:, NP : 2 * NP])
+        wf_bf = late[:, 0:NP].bitcast(BF16).rearrange("p (g n t) -> p g n t", g=2, t=4)
         for g in range(2):
             gp_scale(wf_bf[:, g], wf_raw[:, 4 * g : 4 * g + 4, :].rearrange("p t n -> p n t"), 1.0)
         wf_q = sbuf([P, 2 * N], U32, "wf_q", "w4_sc")
@@ -358,7 +386,7 @@ def tile_list_gnss_spoofing_monitor_kernel(
             energy(s, 0, NP)
             if s == 2:
                 nc.vector.quantize_mx(
-                    out=wf_q[:].bitcast(FP8X4), scales=wf_sc[:], in_=wf_bf[:].rearrange("p g n t -> p (g n t)")
+                    out=wf_q[:].bitcast(FP8X4), scales=wf_sc[:], in_=late[:, 0:NP].bitcast(BF16)
                 )
             if s == 5:
                 weave(nc.vector.tensor_copy, 0, 0, QUARTER, woven=sbuf([P, NP], BF16, "h_bf_first", "page2")[:])

@@ -49,15 +49,13 @@ def tile_list_gnss_spoofing_monitor_kernel(
         fresh_list = lists.tile([P, S // 16], U16, name="fresh_list")
         suspect_list = lists.tile([P, NP // 16], U16, name="suspect_list")
         tab_sc = sbuf([P, T], U8, "tab_sc")
-        for quad in range(4):
-            engine = nc.gpsimd if quad < 3 else nc.vector
-            engine.memset(tab_sc[32 * quad : 32 * quad + 24, :].bitcast(I32), 0)
+        nc.vector.memset(tab_sc[0:96, :].bitcast(I32), 0)
         v_sc = [sbuf([P, NP], U8, "v_sc%d" % a) for a in range(2)]
         for a in range(2):
-            nc.vector.memset(v_sc[a][96:P, :].bitcast(I32), 0)
+            nc.vector.memset(v_sc[a][:].bitcast(I32), 0)
         w4_sc_raw = sbuf([P, 2, H], U8, "w4_sc_raw")
         w4_sc = sbuf([P, 2, H], U8, "w4_sc")
-        nc.vector.memset(w4_sc[:].bitcast(I32), 0)
+        nc.vector.memset(w4_sc_raw[:].bitcast(I32), 0)
         rows = sbuf([P, P], F32, "rows")
         for lo, hi in ((0, ROW0), (32, 64), (64, P)):
             nc.vector.memset(rows[lo:hi, :], 0.0)
@@ -107,12 +105,8 @@ def tile_list_gnss_spoofing_monitor_kernel(
             nc.sync.dma_start(wr[:], w1[:, 512 * g : 512 * (g + 1)].rearrange("(p j) c -> p j c", j=4))
             w1_raw.append(wr)
 
+        nc.sync.dma_start(tab_sc[96:P, :].bitcast(I32), tab_scales.rearrange("a q t -> (a q) t").bitcast(I32))
         nc.sync.dma_start(tab_list[:], offs)
-        for quad in range(4):
-            nc.sync.dma_start(
-                tab_sc[32 * quad + 24 : 32 * quad + 32, :].bitcast(I32),
-                tab_scales[:, 4 * quad : 4 * quad + 4, :].bitcast(I32),
-            )
         nc.sync.dma_start(fresh_list[:], offs2)
         load_plane(SCATTER_ORDER[0], 1)
         for piece in range(1, S // FIRST_PIECE):
@@ -163,22 +157,22 @@ def tile_list_gnss_spoofing_monitor_kernel(
 
         v_sc_rows = sbuf([P, NP], U8, "v_sc_rows")
         nc.vector.tensor_copy(v_sc_rows[:], tab_sc[:].indirect(tab_list[:]))
-        for a in range(2):
-            first_row = 24 + 4 * a
-            nc.gpsimd.dma_start(v_sc[a][0 : P - first_row, :].bitcast(I32), v_sc_rows[first_row:P, :].bitcast(I32))
+        for a, quad in product(range(2), range(4)):
+            first_row = 96 + 16 * a + 4 * quad
+            nc.gpsimd.dma_start(
+                v_sc[a][32 * quad : 32 * quad + 4, :].bitcast(I32), v_sc_rows[first_row : first_row + 4, :].bitcast(I32)
+            )
         scatter(SCATTER_ORDER[0])
         cast_plane(SCATTER_ORDER[0])
         v_w = [sbuf([P, NP], U32, "v_w%d" % a) for a in range(2)]
         for a in range(2):
             nc.vector.tensor_copy(v_w[a][:], tab_w[a][:].indirect(tab_list[:]))
         w4_p = sbuf([P, 2, 2 * H], U8, "w4_p")
-        for quad in range(4):
-            live = slice(32 * quad, 32 * quad + 4)
-            nc.gpsimd.tensor_copy(
-                w4_sc[live].bitcast(I32).rearrange("p a (g t q w) -> p (a g) t q w", g=2, t=4, w=2),
-                w4_sc_raw[live].bitcast(I32).rearrange("p a (g q t w) -> p (a g) t q w", g=2, t=4, w=2),
-            )
-        nc.gpsimd.tensor_copy(
+        nc.vector.tensor_copy(
+            w4_sc[:].bitcast(I32).rearrange("p a (g t q w) -> p (a g) t q w", g=2, t=4, w=2),
+            w4_sc_raw[:].bitcast(I32).rearrange("p a (g q t w) -> p (a g) t q w", g=2, t=4, w=2),
+        )
+        nc.vector.tensor_copy(
             w4_p[:].bitcast(I32).rearrange("p a (g t q w) -> p (a g) t q w", g=2, t=4, w=4),
             w4_raw[:].bitcast(I32).rearrange("p a (g q t w) -> p (a g) t q w", g=2, t=4, w=4),
         )

@@ -22,12 +22,11 @@ P = 128
 BANK = 512
 SCATTER_ORDER = (0, 2, 3, 1)
 END_CHUNKS = ((0, 256), (256, 768), (768, 1024))
-EARLY_GAINS = 5
-QUARTER = 256
+HELD_GAINS = 2
+WEAVE_CUTS = (0, 384, 704, 1024)
 ROW0 = 22
-STAGED_TILES = 2
 FIRST_PIECE = 512
-ON_VECTOR = tuple((s, 3) for s in range(6))
+ON_VECTOR = ((1, 2),) + tuple((s, 3) for s in (0, 1, 2, 3, 4, 6))
 
 
 def tile_list_gnss_spoofing_monitor_kernel(
@@ -45,6 +44,9 @@ def tile_list_gnss_spoofing_monitor_kernel(
         def gp_scale(dst, src, factor):
             nc.gpsimd.tensor_scalar(dst, src, factor, 0.0, ALU.mult, ALU.add)
 
+        def gp_cast(dst, src):
+            gp_scale(dst, src, 1.0)
+
         tab_list = lists.tile([P, NP // 16], U16, name="tab_list")
         fresh_list = lists.tile([P, S // 16], U16, name="fresh_list")
         suspect_list = lists.tile([P, NP // 16], U16, name="suspect_list")
@@ -61,6 +63,8 @@ def tile_list_gnss_spoofing_monitor_kernel(
             nc.vector.memset(rows[lo:hi, :], 0.0)
         ident = sbuf([P, P], F32, "ident")
         make_identity(nc, ident[:])
+        warm = sbuf([P, 8], F32, "warm")
+        nc.scalar.activation(warm[:, 0:1], ident[:, 0:1], ACT.Ln, bias=1.0)
 
         base_planes = base.rearrange("(p t) c -> t p c", t=4)
         xs_planes = xs.rearrange("(p t) c -> t p c", t=4)
@@ -68,7 +72,7 @@ def tile_list_gnss_spoofing_monitor_kernel(
         fresh = {}
 
         def cuts(t):
-            if t == SCATTER_ORDER[0]:
+            if t in (SCATTER_ORDER[0], SCATTER_ORDER[2]):
                 return [(FIRST_PIECE * i, FIRST_PIECE * (i + 1)) for i in range(S // FIRST_PIECE)]
             if t != SCATTER_ORDER[3]:
                 return [(0, S // 4), (S // 4, S)]
@@ -91,19 +95,26 @@ def tile_list_gnss_spoofing_monitor_kernel(
             for lo, hi in cuts(t):
                 nc.vector.tensor_copy(page[t][:].indirect(fresh_list[:, lo // 16 : hi // 16]), fresh[t][:, lo:hi])
 
-        tab_w = [sbuf([P, T], U32, "tab_w%d" % a) for a in range(2)]
+        tab_tile = sbuf([P, 2 * T], U32, "tab_w")
+        tab_w = [tab_tile[:, T * a : T * (a + 1)] for a in range(2)]
 
         def load_table(a, half):
             words = tab_words[a].rearrange("p t i -> p (t i)").bitcast(I32)
             cols = slice(T // 2 * half, T // 2 * (half + 1))
             nc.sync.dma_start(tab_w[a][:, cols].bitcast(I32), words[:, cols])
 
-        w1_raw = []
+        pairs_tile = sbuf([P, 16 * BANK], BF16, "pairs")
+        pairs = [pairs_tile[:, 4 * BANK * c : 4 * BANK * (c + 1)] for c in range(4)]
+        w1_raw = [
+            pairs_tile[:].bitcast(F32).rearrange("p (j half n) -> p j half n", j=4, half=2)[:, :, 1, :],
+            sbuf([P, 4, 512], F32, "w1_raw1")[:],
+        ]
 
-        def load_w1(g):
-            wr = sbuf([P, 4, 512], F32, "w1_raw%d" % g)
-            nc.sync.dma_start(wr[:], w1[:, 512 * g : 512 * (g + 1)].rearrange("(p j) c -> p j c", j=4))
-            w1_raw.append(wr)
+        def load_w1(g, pieces):
+            rows_by_value = w1[:, 512 * g : 512 * (g + 1)].rearrange("(p j) c -> p j c", j=4)
+            step = 4 // pieces
+            for j in range(0, 4, step):
+                nc.sync.dma_start(w1_raw[g][:, j : j + step], rows_by_value[:, j : j + step])
 
         nc.sync.dma_start(tab_sc[96:P, :].bitcast(I32), tab_scales.rearrange("a q t -> (a q) t").bitcast(I32))
         nc.sync.dma_start(tab_list[:], offs)
@@ -135,25 +146,27 @@ def tile_list_gnss_spoofing_monitor_kernel(
             load_table(*divmod(k, 2))
         load_plane(SCATTER_ORDER[1], 1)
         load_fresh(SCATTER_ORDER[1], 1)
+        load_w1(0, 1)
         load_plane(SCATTER_ORDER[2], 1)
-        load_w1(0)
+        load_w1(1, 4)
         load_fresh(SCATTER_ORDER[2], 1)
         load_plane(SCATTER_ORDER[3], 1)
         nc.sync.dma_start(suspect_list[:], offs3)
-        load_w1(1)
-
-        pairs_tile = sbuf([P, 16 * BANK], BF16, "pairs")
-        pairs = [pairs_tile[:, 4 * BANK * c : 4 * BANK * (c + 1)] for c in range(4)]
+        wf_rows = wf.rearrange("(g q t r) n -> g t q r n", g=2, t=4, r=8)
+        wf_raw = sbuf([P, 8, N], F32, "wf_raw")
+        for k in range(8):
+            nc.sync.dma_start(wf_raw[:, k, :], wf_rows[k // 4, k % 4])
 
         def cast_plane(t):
-            for c in range(4):
-                first = 2 * BANK * (t // 2)
-                dst = pairs[c][:, first + t % 2 : first + 2 * BANK : 2]
-                src = page[t][:, BANK * c : BANK * (c + 1)]
-                if t < 2:
-                    nc.scalar.copy(dst, src)
-                else:
-                    gp_scale(dst, src, 1.0)
+            dst = pairs_tile[:].rearrange("p (c u n e) -> p c u n e", c=4, u=2, e=2)[:, :, t // 2, :, t % 2]
+            src = page[t][:].rearrange("p (c n) -> p c n", c=4)
+            if t == SCATTER_ORDER[0]:
+                nc.scalar.copy(dst, src)
+            elif t == SCATTER_ORDER[3]:
+                for c in range(4):
+                    nc.scalar.copy(dst[:, c], src[:, c])
+            else:
+                gp_scale(dst, src, 1.0)
 
         v_sc_rows = sbuf([P, NP], U8, "v_sc_rows")
         nc.vector.tensor_copy(v_sc_rows[:], tab_sc[:].indirect(tab_list[:]))
@@ -165,8 +178,11 @@ def tile_list_gnss_spoofing_monitor_kernel(
         scatter(SCATTER_ORDER[0])
         cast_plane(SCATTER_ORDER[0])
         v_w = [sbuf([P, NP], U32, "v_w%d" % a) for a in range(2)]
-        for a in range(2):
-            nc.vector.tensor_copy(v_w[a][:], tab_w[a][:].indirect(tab_list[:]))
+        nc.vector.tensor_copy(v_w[0][:], tab_w[0].indirect(tab_list[:]))
+        for lo in (0, BANK):
+            nc.vector.tensor_copy(
+                v_w[1][:, lo : lo + BANK], tab_w[1].indirect(tab_list[:, lo // 16 : (lo + BANK) // 16])
+            )
         w4_p = sbuf([P, 2, 2 * H], U8, "w4_p")
         nc.vector.tensor_copy(
             w4_sc[:].bitcast(I32).rearrange("p a (g t q w) -> p (a g) t q w", g=2, t=4, w=2),
@@ -207,87 +223,75 @@ def tile_list_gnss_spoofing_monitor_kernel(
                         stop=(a == 1),
                     )
                 nc.scalar.activation(plane(log_b, s, BANK * half, BANK * (half + 1)), acc[:], ACT.Square)
-            nc.scalar.activation(by_halves(logs(s)), by_halves(plane(log_b, s)), ACT.Ln, bias=1.0)
+            nc.scalar.activation(plane(log_b, s), plane(log_b, s), ACT.Ln, bias=1.0)
 
-        def by_halves(values):
-            return values if values.ndim == 3 else values.rearrange("p (u n) -> p u n", u=2)
+        def record_gain(s, dst):
+            gained_b[s] = dst
+            gp_scale(dst, plane(log_b, s), gain_col[:, s : s + 1])
 
-        def logs(s):
-            if s >= STAGED_TILES:
-                return plane(log_b, s)
-            words = pairs_tile[:].bitcast(F32).rearrange("p (c half n) -> p c half n", c=4, half=2)
-            return words[:, 2 * s : 2 * s + 2, 1, :]
-
-        def record_gain(s, dst=None):
-            gained_b[s] = plane(log_b, s % EARLY_GAINS) if dst is None else dst
-            gp_scale(by_halves(gained_b[s]), by_halves(logs(s)), gain_col[:, s : s + 1])
-
-        w1_bf = {}
+        page_bf = sbuf([P, 20 * BANK], BF16, "page_bf")
+        w1_bf = [sbuf([P, 4 * BANK], BF16, "w1_bf0")[:], page_bf[:, 16 * BANK : 20 * BANK]]
         w1_q = {}
         w1_sc = sbuf([P, H], U8, "w1_sc")
 
-        def cast_w1(g):
-            w1_bf[g] = sbuf([P, 4, P, 4], BF16, "w1_bf%d" % g)
-            by_tile = w1_raw[g][:].rearrange("p j (q t r) -> p t q r j", t=4, r=8)
-            for t in range(4):
-                gp_scale(w1_bf[g][:, t, :, :].rearrange("p (q r) j -> p q r j", r=8), by_tile[:, t], 1.0)
+        def cast_w1(g, tiles, copy):
+            by_tile = w1_raw[g].rearrange("p j (q t r) -> p t q r j", t=4, r=8)
+            woven = w1_bf[g].rearrange("p (t q r j) -> p t q r j", t=4, r=8, j=4)
+            for t in tiles:
+                copy(woven[:, t], by_tile[:, t])
 
         def quantise_w1(g):
             cols = slice(512 * g, 512 * (g + 1))
-            w1_q[g] = sbuf([P, 512], U32, "w1_q%d" % g, ("fresh%d" % SCATTER_ORDER[3], "page_bf2")[g])
+            w1_q[g] = sbuf([P, 512], U32, "w1_q%d" % g, ("fresh%d" % SCATTER_ORDER[3], "pairs")[g])
             nc.vector.quantize_mx(
                 out=w1_q[g][:].bitcast(FP8X4), scales=w1_sc[:, cols],
-                in_=w1_bf[g][:].rearrange("p t m j -> p (t m j)"),
+                in_=w1_bf[g],
             )
 
         gained_b = {}
-        wf_rows = wf.rearrange("(g q t r) n -> g t q r n", g=2, t=4, r=8)
         for s in range(8):
-            if s == 7:
-                cast_plane(SCATTER_ORDER[3])
             record_tile(s)
-            if s < EARLY_GAINS - 1:
-                record_gain(s)
-            if s == STAGED_TILES - 1:
+            if s == 0:
+                record_gain(s, plane(log_b, s))
+                cast_w1(0, range(4), gp_cast)
                 cast_plane(SCATTER_ORDER[1])
-                cast_w1(0)
-                wf_raw = sbuf([P, 8, N], F32, "wf_raw", "w1_raw0")
-                for k in range(8):
-                    nc.sync.dma_start(wf_raw[:, k, :], wf_rows[k // 4, k % 4])
+                cast_w1(1, (0, 1), gp_cast)
                 cast_plane(SCATTER_ORDER[2])
+        cast_w1(1, (2, 3), nc.scalar.copy)
+        cast_plane(SCATTER_ORDER[3])
         quantise_w1(0)
 
         page_q = [sbuf([P, BANK], U32, "page_q%d" % c) for c in range(4)]
         page_sc = [sbuf([P, BANK], U8, "page_sc%d" % c) for c in range(4)]
-        page_bf = []
         for c in range(5):
             if c < 4:
-                pb = sbuf([P, BANK, 4], BF16, "page_bf%d" % c)
                 nc.vector.tensor_copy(
-                    pb[:].rearrange("p n t -> p (n t)").bitcast(I32).rearrange("p (n i u) -> p n u i", u=2, i=2),
+                    page_bf[:, 4 * BANK * c : 4 * BANK * (c + 1)]
+                    .bitcast(I32)
+                    .rearrange("p (n i u) -> p n u i", u=2, i=2),
                     pairs[c].bitcast(I32).rearrange("p (u n i) -> p n u i", u=2, i=2),
                 )
-                page_bf.append(pb)
             if c > 0:
                 nc.vector.quantize_mx(
                     out=page_q[c - 1][:].bitcast(FP8X4), scales=page_sc[c - 1][:],
-                    in_=page_bf[c - 1][:].rearrange("p n t -> p (n t)"),
+                    in_=page_bf[:, 4 * BANK * (c - 1) : 4 * BANK * c],
                 )
-        w1_bf[1] = sbuf([P, 4, P, 4], BF16, "w1_bf1", "page_bf3")
-        nc.vector.tensor_copy(
-            w1_bf[1][:].rearrange("p t (q r) j -> p t q r j", r=8),
-            w1_raw[1][:].rearrange("p j (q t r) -> p t q r j", t=4, r=8),
-        )
         quantise_w1(1)
-        late = sbuf([P, 2 * NP], F32, "late", "page_bf3")
-        record_gain(EARLY_GAINS - 1, late[:, NP : 2 * NP])
-        wf_bf = late[:, 0:NP].bitcast(BF16).rearrange("p (g n t) -> p g n t", g=2, t=4)
-        for g in range(2):
-            gp_scale(wf_bf[:, g], wf_raw[:, 4 * g : 4 * g + 4, :].rearrange("p t n -> p n t"), 1.0)
+        late = sbuf([P, 4 * NP], F32, "late", "page_bf")
+        for k in range(HELD_GAINS):
+            record_gain(1 + k, late[:, NP * (k + 1) : NP * (k + 2)])
+        gp_scale(
+            late[:, 0:NP].bitcast(BF16).rearrange("p (g n t) -> p g n t", g=2, t=4),
+            wf_raw[:].rearrange("p (g t) n -> p g n t", g=2),
+            1.0,
+        )
         wf_q = sbuf([P, 2 * N], U32, "wf_q", "w4_sc")
         wf_sc = sbuf([P, 2 * N], U8, "wf_sc")
 
-        log_a = [sbuf([P, 4 * NP], F32, "log_a%d" % g, "tab_w%d" % g) for g in range(2)]
+        log_a_tile = sbuf([P, 8 * NP], F32, "log_a", "tab_w")
+        log_a = [log_a_tile[:, 4 * NP * g : 4 * NP * (g + 1)] for g in range(2)]
+        woven_start = 4 * NP - 2 * WEAVE_CUTS[1]
+        woven_first = log_a_tile[:, woven_start : woven_start + 2 * NP].bitcast(BF16)
         proj = {}
         h_q = {1: sbuf([P, NP], U32, "h_q1")}
         h_sc = [sbuf([P, NP], U8, "h_sc%d" % g) for g in range(2)]
@@ -320,7 +324,7 @@ def tile_list_gnss_spoofing_monitor_kernel(
             nc.scalar.activation(part, part, ACT.Square)
             nc.scalar.activation(part, part, ACT.Ln, bias=1.0)
 
-        h_planes = [sbuf([P, 4 * NP], BF16, "h_planes%d" % g, ("pairs", "w1_raw1")[g]) for g in range(2)]
+        h_planes = [sbuf([P, 4 * NP], BF16, "h_planes%d" % g, ("tab_sc", "w1_raw1")[g]) for g in range(2)]
 
         def compare(s, lo, hi):
             nc.vector.scalar_tensor_tensor(
@@ -366,7 +370,7 @@ def tile_list_gnss_spoofing_monitor_kernel(
             for h in range(2):
                 acc = acc_y[lo, h][:, 0 : hi - lo]
                 staged = staged_tile[:, NP * h + lo : NP * h + hi]
-                if h == 1 and hi == NP:
+                if h == 1 and (lo, hi) == END_CHUNKS[1]:
                     nc.vector.tensor_scalar_add(staged, acc, minus_thr[:, h : h + 1])
                 else:
                     nc.scalar.activation(staged, acc, ACT.Identity, bias=minus_thr[:, h : h + 1])
@@ -382,21 +386,21 @@ def tile_list_gnss_spoofing_monitor_kernel(
                 nc.vector.quantize_mx(
                     out=wf_q[:].bitcast(FP8X4), scales=wf_sc[:], in_=late[:, 0:NP].bitcast(BF16)
                 )
-            if s == 5:
-                weave(nc.vector.tensor_copy, 0, 0, QUARTER, woven=sbuf([P, NP], BF16, "h_bf_first", "page2")[:])
             if s == 6:
                 h_q[0] = sbuf([P, NP], U32, "h_q0", "page3")
-                for k in (0, 1):
-                    quantise_h(0, QUARTER * k, QUARTER * (k + 1))
+                h_bf[0, 0] = woven_first[:, 0 : 2 * NP]
+                h_bf[0, NP // 2] = woven_first[:, 2 * NP : 4 * NP]
+                quantise_h(0, 0, NP // 2)
             if s >= 1:
                 compare(s - 1, 0, NP)
             if s >= 4:
-                lo = QUARTER * (s - 3)
-                released = gained_b[s - 1][:, 0 : NP // 2].bitcast(BF16)
-                weave(lambda dst, src: gp_scale(dst, src, 1.0), 0, lo, lo + QUARTER, 1, 1, released)
-            if 1 <= s <= 8 - EARLY_GAINS:
-                record_gain(EARLY_GAINS + s - 1)
-        staged_tile = sbuf([P, 2 * NP], F32, "staged", "w1_raw0")
+                lo, hi = WEAVE_CUTS[s - 4 : s - 2]
+                weave(gp_cast, 0, lo, hi, 1, 1, woven_first[:, 4 * lo : 4 * hi])
+            if 1 <= s <= 3:
+                record_gain(2 * s + 1, gained_b[s - 1])
+            if 1 <= s <= 2:
+                record_gain(2 * s + 2, plane(log_a, s - 1))
+        staged_tile = sbuf([P, 2 * NP], F32, "staged", "wf_raw")
         first, second, last = END_CHUNKS
         for chunk in END_CHUNKS:
             pick(7, *chunk)
@@ -405,13 +409,12 @@ def tile_list_gnss_spoofing_monitor_kernel(
         for chunk in END_CHUNKS:
             compare(7, *chunk)
         weave(nc.scalar.copy, 1, *first)
-        for k in (2, 3):
-            quantise_h(0, QUARTER * k, QUARTER * (k + 1))
+        quantise_h(0, NP // 2, NP)
         for chunk in END_CHUNKS:
             alarm_pass(0, *chunk)
+        weave(nc.scalar.copy, 1, *last)
         weave(nc.vector.tensor_copy, 1, *second)
-        weave(nc.vector.tensor_copy, 1, *last)
-        for chunk in END_CHUNKS:
+        for chunk in (first, last, second):
             quantise_h(1, *chunk)
             alarm_pass(1, *chunk)
             store(*chunk)

@@ -22,11 +22,12 @@ P = 128
 BANK = 512
 SCATTER_ORDER = (0, 2, 3, 1)
 END_CHUNKS = ((0, 256), (256, 768), (768, 1024))
-HELD_GAINS = 2
-WEAVE_CUTS = (0, 384, 704, 1024)
+HELD_GAINS = 3
+WEAVE_CUTS = (0, 320, 672, 1024)
 ROW0 = 22
+QUARTER = 256
 FIRST_PIECE = 512
-ON_VECTOR = ((1, 2),) + tuple((s, 3) for s in (0, 1, 2, 3, 4, 6))
+LAST_BANK_ON_VECTOR = (0, 2, 3, 4, 6)
 
 
 def tile_list_gnss_spoofing_monitor_kernel(
@@ -64,7 +65,7 @@ def tile_list_gnss_spoofing_monitor_kernel(
         ident = sbuf([P, P], F32, "ident")
         make_identity(nc, ident[:])
         warm = sbuf([P, 8], F32, "warm")
-        nc.scalar.activation(warm[:, 0:1], ident[:, 0:1], ACT.Ln, bias=1.0)
+        nc.scalar.activation(warm[64:P, 0:1], rows[64:P, 0:1], ACT.Ln, bias=1.0)
 
         base_planes = base.rearrange("(p t) c -> t p c", t=4)
         xs_planes = xs.rearrange("(p t) c -> t p c", t=4)
@@ -72,11 +73,9 @@ def tile_list_gnss_spoofing_monitor_kernel(
         fresh = {}
 
         def cuts(t):
-            if t in (SCATTER_ORDER[0], SCATTER_ORDER[2]):
+            if t != SCATTER_ORDER[1]:
                 return [(FIRST_PIECE * i, FIRST_PIECE * (i + 1)) for i in range(S // FIRST_PIECE)]
-            if t != SCATTER_ORDER[3]:
-                return [(0, S // 4), (S // 4, S)]
-            return [(0, S)]
+            return [(0, S // 4), (S // 4, S)]
 
         def load_plane(t, pieces):
             page[t] = sbuf([P, T2], F32, "page%d" % t)
@@ -151,6 +150,7 @@ def tile_list_gnss_spoofing_monitor_kernel(
         load_w1(1, 4)
         load_fresh(SCATTER_ORDER[2], 1)
         load_plane(SCATTER_ORDER[3], 1)
+        load_fresh(SCATTER_ORDER[3], 1)
         nc.sync.dma_start(suspect_list[:], offs3)
         wf_rows = wf.rearrange("(g q t r) n -> g t q r n", g=2, t=4, r=8)
         wf_raw = sbuf([P, 8, N], F32, "wf_raw")
@@ -251,8 +251,9 @@ def tile_list_gnss_spoofing_monitor_kernel(
         gained_b = {}
         for s in range(8):
             record_tile(s)
-            if s == 0:
+            if s < 2:
                 record_gain(s, plane(log_b, s))
+            if s == 1:
                 cast_w1(0, range(4), gp_cast)
                 cast_plane(SCATTER_ORDER[1])
                 cast_w1(1, (0, 1), gp_cast)
@@ -279,20 +280,19 @@ def tile_list_gnss_spoofing_monitor_kernel(
         quantise_w1(1)
         late = sbuf([P, 4 * NP], F32, "late", "page_bf")
         for k in range(HELD_GAINS):
-            record_gain(1 + k, late[:, NP * (k + 1) : NP * (k + 2)])
+            record_gain(2 + k, late[:, NP * (k + 1) : NP * (k + 2)])
         gp_scale(
             late[:, 0:NP].bitcast(BF16).rearrange("p (g n t) -> p g n t", g=2, t=4),
             wf_raw[:].rearrange("p (g t) n -> p g n t", g=2),
             1.0,
         )
-        wf_q = sbuf([P, 2 * N], U32, "wf_q", "w4_sc")
-        wf_sc = sbuf([P, 2 * N], U8, "wf_sc")
 
         log_a_tile = sbuf([P, 8 * NP], F32, "log_a", "tab_w")
         log_a = [log_a_tile[:, 4 * NP * g : 4 * NP * (g + 1)] for g in range(2)]
-        woven_start = 4 * NP - 2 * WEAVE_CUTS[1]
+        woven_start = 4 * NP - 2 * WEAVE_CUTS[2]
         woven_first = log_a_tile[:, woven_start : woven_start + 2 * NP].bitcast(BF16)
         proj = {}
+        last_bank = {}
         h_q = {1: sbuf([P, NP], U32, "h_q1")}
         h_sc = [sbuf([P, NP], U8, "h_sc%d" % g) for g in range(2)]
         h_bf = {}
@@ -311,10 +311,14 @@ def tile_list_gnss_spoofing_monitor_kernel(
                     start=True,
                     stop=True,
                 )
-                if (s, c) in ON_VECTOR:
-                    nc.vector.tensor_copy(proj[s][:, BANK * c : BANK * (c + 1)], acc[:])
+                if c == 3 and s in LAST_BANK_ON_VECTOR:
+                    last_bank[s] = acc
                 else:
                     nc.scalar.copy(proj[s][:, BANK * c : BANK * (c + 1)], acc[:])
+
+        def empty_last_bank(s):
+            if s in LAST_BANK_ON_VECTOR:
+                nc.vector.tensor_copy(proj[s][:, 3 * BANK : 4 * BANK], last_bank[s][:])
 
         def pick(s, lo, hi):
             nc.vector.tensor_copy(plane(log_a, s, lo, hi), proj[s][:].indirect(suspect_list[:, lo // 16 : hi // 16]))
@@ -370,7 +374,7 @@ def tile_list_gnss_spoofing_monitor_kernel(
             for h in range(2):
                 acc = acc_y[lo, h][:, 0 : hi - lo]
                 staged = staged_tile[:, NP * h + lo : NP * h + hi]
-                if h == 1 and (lo, hi) == END_CHUNKS[1]:
+                if h == 1 and lo >= NP // 2:
                     nc.vector.tensor_scalar_add(staged, acc, minus_thr[:, h : h + 1])
                 else:
                     nc.scalar.activation(staged, acc, ACT.Identity, bias=minus_thr[:, h : h + 1])
@@ -378,11 +382,14 @@ def tile_list_gnss_spoofing_monitor_kernel(
 
         project((0, 1))
         for s in range(7):
-            if s >= 1:
-                project((s + 1,))
+            if s < 6:
+                project((s + 2,))
+            empty_last_bank(s + 1 if s else 0)
             pick(s, 0, NP)
             energy(s, 0, NP)
-            if s == 2:
+            if s == 5:
+                wf_q = sbuf([P, 2 * N], U32, "wf_q", "page2")
+                wf_sc = sbuf([P, 2 * N], U8, "wf_sc")
                 nc.vector.quantize_mx(
                     out=wf_q[:].bitcast(FP8X4), scales=wf_sc[:], in_=late[:, 0:NP].bitcast(BF16)
                 )
@@ -393,28 +400,30 @@ def tile_list_gnss_spoofing_monitor_kernel(
                 quantise_h(0, 0, NP // 2)
             if s >= 1:
                 compare(s - 1, 0, NP)
-            if s >= 4:
-                lo, hi = WEAVE_CUTS[s - 4 : s - 2]
+            if s == 5:
+                lo, hi = WEAVE_CUTS[0:2]
+                weave(nc.scalar.copy, 0, lo, hi, woven=woven_first[:, 4 * lo : 4 * hi])
+            if s in (4, 5):
+                lo, hi = WEAVE_CUTS[s - 3 : s - 1]
                 weave(gp_cast, 0, lo, hi, 1, 1, woven_first[:, 4 * lo : 4 * hi])
             if 1 <= s <= 3:
-                record_gain(2 * s + 1, gained_b[s - 1])
-            if 1 <= s <= 2:
-                record_gain(2 * s + 2, plane(log_a, s - 1))
+                record_gain(s + 4, gained_b[s - 1])
         staged_tile = sbuf([P, 2 * NP], F32, "staged", "wf_raw")
-        first, second, last = END_CHUNKS
         for chunk in END_CHUNKS:
             pick(7, *chunk)
             energy(7, *chunk)
         compare(6, 0, NP)
         for chunk in END_CHUNKS:
             compare(7, *chunk)
-        weave(nc.scalar.copy, 1, *first)
+        quarters = [(QUARTER * k, QUARTER * (k + 1)) for k in range(4)]
+        weave(nc.scalar.copy, 1, *quarters[0])
+        weave(nc.scalar.copy, 1, *quarters[3])
         quantise_h(0, NP // 2, NP)
-        for chunk in END_CHUNKS:
-            alarm_pass(0, *chunk)
-        weave(nc.scalar.copy, 1, *last)
-        weave(nc.vector.tensor_copy, 1, *second)
-        for chunk in (first, last, second):
-            quantise_h(1, *chunk)
-            alarm_pass(1, *chunk)
-            store(*chunk)
+        for cols in quarters:
+            alarm_pass(0, *cols)
+        for woven_next, finished in ((1, 0), (2, 1), (None, 3), (None, 2)):
+            if woven_next is not None:
+                weave(nc.vector.tensor_copy, 1, *quarters[woven_next])
+            quantise_h(1, *quarters[finished])
+            alarm_pass(1, *quarters[finished])
+            store(*quarters[finished])

@@ -64,8 +64,6 @@ def tile_list_gnss_spoofing_monitor_kernel(
             nc.vector.memset(rows[lo:hi, :], 0.0)
         ident = sbuf([P, P], F32, "ident")
         make_identity(nc, ident[:])
-        warm = sbuf([P, 8], F32, "warm")
-        nc.scalar.activation(warm[64:P, 0:1], rows[64:P, 0:1], ACT.Ln, bias=1.0)
 
         base_planes = base.rearrange("(p t) c -> t p c", t=4)
         xs_planes = xs.rearrange("(p t) c -> t p c", t=4)

@@ -62,6 +62,12 @@ def tile_list_gnss_spoofing_monitor_kernel(
         rows = sbuf([P, P], F32, "rows")
         for lo, hi in ((0, ROW0), (32, 64), (64, P)):
             nc.vector.memset(rows[lo:hi, :], 0.0)
+        for g in range(2):
+            nc.gpsimd.dma_start(
+                rows[ROW0 + 4 * g : ROW0 + 4 * g + 4, :].rearrange("t (q r) -> t q r", r=8),
+                gain[512 * g : 512 * (g + 1)].rearrange("(q t r) -> t q r", t=4, r=8),
+            )
+        nc.gpsimd.dma_start(rows[ROW0 + 8 : ROW0 + 10, :], thr.rearrange("(h p) -> h p", h=2))
         ident = sbuf([P, P], F32, "ident")
         make_identity(nc, ident[:])
 
@@ -126,14 +132,6 @@ def tile_list_gnss_spoofing_monitor_kernel(
             )
             for quad in range(4)
         ]
-        small_loads += [
-            (
-                rows[ROW0 + 4 * g : ROW0 + 4 * g + 4, :].rearrange("t (q r) -> t q r", r=8),
-                gain[512 * g : 512 * (g + 1)].rearrange("(q t r) -> t q r", t=4, r=8),
-            )
-            for g in range(2)
-        ]
-        small_loads += [(rows[ROW0 + 8 : ROW0 + 10, :], thr.rearrange("(h p) -> h p", h=2))]
         w4_raw = sbuf([P, 2, 2 * H], U8, "w4_raw")
         for k in range(4):
             for dst, src in small_loads[2 * k : 2 * k + 2]:

from contextlib import ExitStack
from itertools import product

import concourse.mybir as mybir
from concourse.masks import make_identity

K, K2, T, T2, S, NP, H, N = 1024, 512, 4096, 2048, 1024, 1024, 1024, 256
FLOPS = 2 * (K2 * H * T2 + K * H * NP + H * N * NP)

F32 = mybir.dt.float32
BF16 = mybir.dt.bfloat16
I32 = mybir.dt.int32
U32 = mybir.dt.uint32
U16 = mybir.dt.uint16
U8 = mybir.dt.uint8
FP8X4 = mybir.dt.float8_e4m3fn_x4
FP4X4 = mybir.dt.float4_e2m1fn_x4
ACT = mybir.ActivationFunctionType
ALU = mybir.AluOpType

P = 128
BANK = 512
SCATTER_ORDER = (0, 2, 3, 1)
END_CHUNKS = ((0, 256), (256, 768), (768, 1024))
HELD_GAINS = 3
WEAVE_CUTS = (0, 320, 672, 1024)
ROW0 = 22
QUARTER = 256
FIRST_PIECE = 512
LAST_BANK_ON_VECTOR = (0, 2, 3, 4, 6)


def tile_list_gnss_spoofing_monitor_kernel(
    tc, tab_words, tab_scales, w4_words, w4_scales, base, xs, w1, gain, wf, thr, offs, offs2, offs3, out
):
    nc = tc.nc
    with ExitStack() as ctx:
        lists = ctx.enter_context(tc.tile_pool(name="lists", bufs=1))
        keep = ctx.enter_context(tc.tile_pool(name="keep", bufs=1))
        psum = ctx.enter_context(tc.psum_pool(name="psum", bufs=8))

        def sbuf(shape, dtype, name, tag=None):
            return keep.tile(shape, dtype, name=name, tag=tag or name, align_bytes=64)

        def gp_scale(dst, src, factor):
            nc.gpsimd.tensor_scalar(dst, src, factor, 0.0, ALU.mult, ALU.add)

        def gp_cast(dst, src):
            gp_scale(dst, src, 1.0)

        tab_list = lists.tile([P, NP // 16], U16, name="tab_list")
        fresh_list = lists.tile([P, S // 16], U16, name="fresh_list")
        suspect_list = lists.tile([P, NP // 16], U16, name="suspect_list")
        tab_sc = sbuf([P, T], U8, "tab_sc")
        nc.vector.memset(tab_sc[0:96, :].bitcast(I32), 0)
        v_sc = [sbuf([P, NP], U8, "v_sc%d" % a) for a in range(2)]
        for a in range(2):
            nc.vector.memset(v_sc[a][:].bitcast(I32), 0)
        w4_sc_raw = sbuf([P, 2, H], U8, "w4_sc_raw")
        w4_sc = sbuf([P, 2, H], U8, "w4_sc")
        nc.vector.memset(w4_sc_raw[:].bitcast(I32), 0)
        rows = sbuf([P, P], F32, "rows")
        for lo, hi in ((0, ROW0), (32, 64), (64, P)):
            nc.vector.memset(rows[lo:hi, :], 0.0)
        for g in range(2):
            nc.gpsimd.dma_start(
                rows[ROW0 + 4 * g : ROW0 + 4 * g + 4, :].rearrange("t (q r) -> t q r", r=8),
                gain[512 * g : 512 * (g + 1)].rearrange("(q t r) -> t q r", t=4, r=8),
            )
        nc.gpsimd.dma_start(rows[ROW0 + 8 : ROW0 + 10, :], thr.rearrange("(h p) -> h p", h=2))
        ident = sbuf([P, P], F32, "ident")
        make_identity(nc, ident[:])

        base_planes = base.rearrange("(p t) c -> t p c", t=4)
        xs_planes = xs.rearrange("(p t) c -> t p c", t=4)
        page = {}
        fresh = {}

        def cuts(t):
            if t != SCATTER_ORDER[1]:
                return [(FIRST_PIECE * i, FIRST_PIECE * (i + 1)) for i in range(S // FIRST_PIECE)]
            return [(0, S // 4), (S // 4, S)]

        def load_plane(t, pieces):
            page[t] = sbuf([P, T2], F32, "page%d" % t)
            fresh[t] = sbuf([P, S], F32, "fresh%d" % t)
            width = T2 // pieces
            for i in range(pieces):
                cols = slice(width * i, width * (i + 1))
                nc.sync.dma_start(page[t][:, cols], base_planes[t][:, cols])
            load_fresh(t, 0)

        def load_fresh(t, piece):
            lo, hi = cuts(t)[piece]
            nc.sync.dma_start(fresh[t][:, lo:hi], xs_planes[t][:, lo:hi])

        def scatter(t):
            for lo, hi in cuts(t):
                nc.vector.tensor_copy(page[t][:].indirect(fresh_list[:, lo // 16 : hi // 16]), fresh[t][:, lo:hi])

        tab_tile = sbuf([P, 2 * T], U32, "tab_w")
        tab_w = [tab_tile[:, T * a : T * (a + 1)] for a in range(2)]

        def load_table(a, half):
            words = tab_words[a].rearrange("p t i -> p (t i)").bitcast(I32)
            cols = slice(T // 2 * half, T // 2 * (half + 1))
            nc.sync.dma_start(tab_w[a][:, cols].bitcast(I32), words[:, cols])

        pairs_tile = sbuf([P, 16 * BANK], BF16, "pairs")
        pairs = [pairs_tile[:, 4 * BANK * c : 4 * BANK * (c + 1)] for c in range(4)]
        w1_raw = [
            pairs_tile[:].bitcast(F32).rearrange("p (j half n) -> p j half n", j=4, half=2)[:, :, 1, :],
            sbuf([P, 4, 512], F32, "w1_raw1")[:],
        ]

        def load_w1(g, pieces):
            rows_by_value = w1[:, 512 * g : 512 * (g + 1)].rearrange("(p j) c -> p j c", j=4)
            step = 4 // pieces
            for j in range(0, 4, step):
                nc.sync.dma_start(w1_raw[g][:, j : j + step], rows_by_value[:, j : j + step])

        nc.sync.dma_start(tab_sc[96:P, :].bitcast(I32), tab_scales.rearrange("a q t -> (a q) t").bitcast(I32))
        nc.sync.dma_start(tab_list[:], offs)
        nc.sync.dma_start(fresh_list[:], offs2)
        load_plane(SCATTER_ORDER[0], 1)
        for piece in range(1, S // FIRST_PIECE):
            load_fresh(SCATTER_ORDER[0], piece)
        small_loads = [
            (
                w4_sc_raw[32 * quad : 32 * quad + 4, :, :].bitcast(I32),
                w4_scales[:, 4 * quad : 4 * quad + 4, :].bitcast(I32).rearrange("a r w -> r a w"),
            )
            for quad in range(4)
        ]
        w4_raw = sbuf([P, 2, 2 * H], U8, "w4_raw")
        for k in range(4):
            for dst, src in small_loads[2 * k : 2 * k + 2]:
                nc.sync.dma_start(dst, src)
            if k == 2:
                nc.sync.dma_start(w4_raw[:].bitcast(I32), w4_words.bitcast(I32).rearrange("a p w -> p a w"))
            load_table(*divmod(k, 2))
        load_plane(SCATTER_ORDER[1], 1)
        load_fresh(SCATTER_ORDER[1], 1)
        load_w1(0, 1)
        load_plane(SCATTER_ORDER[2], 1)
        load_w1(1, 4)
        load_fresh(SCATTER_ORDER[2], 1)
        load_plane(SCATTER_ORDER[3], 1)
        load_fresh(SCATTER_ORDER[3], 1)
        nc.sync.dma_start(suspect_list[:], offs3)
        wf_rows = wf.rearrange("(g q t r) n -> g t q r n", g=2, t=4, r=8)
        wf_raw = sbuf([P, 8, N], F32, "wf_raw")
        for k in range(8):
            nc.sync.dma_start(wf_raw[:, k, :], wf_rows[k // 4, k % 4])

        def cast_plane(t):
            dst = pairs_tile[:].rearrange("p (c u n e) -> p c u n e", c=4, u=2, e=2)[:, :, t // 2, :, t % 2]
            src = page[t][:].rearrange("p (c n) -> p c n", c=4)
            if t == SCATTER_ORDER[0]:
                nc.scalar.copy(dst, src)
            elif t == SCATTER_ORDER[3]:
                for c in range(4):
                    nc.scalar.copy(dst[:, c], src[:, c])
            else:
                gp_scale(dst, src, 1.0)

        v_sc_rows = sbuf([P, NP], U8, "v_sc_rows")
        nc.vector.tensor_copy(v_sc_rows[:], tab_sc[:].indirect(tab_list[:]))
        for a, quad in product(range(2), range(4)):
            first_row = 96 + 16 * a + 4 * quad
            nc.gpsimd.dma_start(
                v_sc[a][32 * quad : 32 * quad + 4, :].bitcast(I32), v_sc_rows[first_row : first_row + 4, :].bitcast(I32)
            )
        scatter(SCATTER_ORDER[0])
        cast_plane(SCATTER_ORDER[0])
        v_w = [sbuf([P, NP], U32, "v_w%d" % a) for a in range(2)]
        nc.vector.tensor_copy(v_w[0][:], tab_w[0].indirect(tab_list[:]))
        for lo in (0, BANK):
            nc.vector.tensor_copy(
                v_w[1][:, lo : lo + BANK], tab_w[1].indirect(tab_list[:, lo // 16 : (lo + BANK) // 16])
            )
        w4_p = sbuf([P, 2, 2 * H], U8, "w4_p")
        nc.vector.tensor_copy(
            w4_sc[:].bitcast(I32).rearrange("p a (g t q w) -> p (a g) t q w", g=2, t=4, w=2),
            w4_sc_raw[:].bitcast(I32).rearrange("p a (g q t w) -> p (a g) t q w", g=2, t=4, w=2),
        )
        nc.vector.tensor_copy(
            w4_p[:].bitcast(I32).rearrange("p a (g t q w) -> p (a g) t q w", g=2, t=4, w=4),
            w4_raw[:].bitcast(I32).rearrange("p a (g q t w) -> p (a g) t q w", g=2, t=4, w=4),
        )
        for t in SCATTER_ORDER[1:]:
            scatter(t)

        turned = psum.tile([P, BANK], F32, name="turned", tag="bank")
        nc.tensor.transpose(turned[:, 0:P], rows[:], ident[:])
        gain_col = sbuf([P, 8], F32, "gain_col")
        nc.scalar.activation(gain_col[:], turned[:, ROW0 : ROW0 + 8], ACT.Copy)
        minus_thr = sbuf([P, 2], F32, "minus_thr")
        nc.scalar.activation(minus_thr[:], turned[:, ROW0 + 8 : ROW0 + 10], ACT.Copy, scale=-1.0)

        log_b = [sbuf([P, 4 * NP], F32, "log_b%d" % g) for g in range(2)]

        def plane(tiles, s, lo=0, hi=NP):
            g, t = divmod(s, 4)
            return tiles[g][:, NP * t + lo : NP * t + hi]

        def record_tile(s):
            for half in range(2):
                acc = psum.tile([P, BANK], F32, name="acc_b", tag="bank")
                cols = slice(BANK * half, BANK * (half + 1))
                for a in range(2):
                    nc.tensor.matmul_mx(
                        out=acc[:],
                        lhsT=w4_p[:, a, 2 * P * s : 2 * P * (s + 1)].bitcast(FP4X4),
                        lhsT_scale=w4_sc[:, a, P * s : P * (s + 1)],
                        rhs=v_w[a][:, cols].bitcast(FP8X4),
                        rhs_scale=v_sc[a][:, cols],
                        start=(a == 0),
                        stop=(a == 1),
                    )
                nc.scalar.activation(plane(log_b, s, BANK * half, BANK * (half + 1)), acc[:], ACT.Square)
            nc.scalar.activation(plane(log_b, s), plane(log_b, s), ACT.Ln, bias=1.0)

        def record_gain(s, dst):
            gained_b[s] = dst
            gp_scale(dst, plane(log_b, s), gain_col[:, s : s + 1])

        page_bf = sbuf([P, 20 * BANK], BF16, "page_bf")
        w1_bf = [sbuf([P, 4 * BANK], BF16, "w1_bf0")[:], page_bf[:, 16 * BANK : 20 * BANK]]
        w1_q = {}
        w1_sc = sbuf([P, H], U8, "w1_sc")

        def cast_w1(g, tiles, copy):
            by_tile = w1_raw[g].rearrange("p j (q t r) -> p t q r j", t=4, r=8)
            woven = w1_bf[g].rearrange("p (t q r j) -> p t q r j", t=4, r=8, j=4)
            for t in tiles:
                copy(woven[:, t], by_tile[:, t])

        def quantise_w1(g):
            cols = slice(512 * g, 512 * (g + 1))
            w1_q[g] = sbuf([P, 512], U32, "w1_q%d" % g, ("fresh%d" % SCATTER_ORDER[3], "pairs")[g])
            nc.vector.quantize_mx(
                out=w1_q[g][:].bitcast(FP8X4), scales=w1_sc[:, cols],
                in_=w1_bf[g],
            )

        gained_b = {}
        for s in range(8):
            record_tile(s)
            if s < 2:
                record_gain(s, plane(log_b, s))
            if s == 1:
                cast_w1(0, range(4), gp_cast)
                cast_plane(SCATTER_ORDER[1])
                cast_w1(1, (0, 1), gp_cast)
                cast_plane(SCATTER_ORDER[2])
        cast_w1(1, (2, 3), nc.scalar.copy)
        cast_plane(SCATTER_ORDER[3])
        quantise_w1(0)

        page_q = [sbuf([P, BANK], U32, "page_q%d" % c) for c in range(4)]
        page_sc = [sbuf([P, BANK], U8, "page_sc%d" % c) for c in range(4)]
        for c in range(5):
            if c < 4:
                nc.vector.tensor_copy(
                    page_bf[:, 4 * BANK * c : 4 * BANK * (c + 1)]
                    .bitcast(I32)
                    .rearrange("p (n i u) -> p n u i", u=2, i=2),
                    pairs[c].bitcast(I32).rearrange("p (u n i) -> p n u i", u=2, i=2),
                )
            if c > 0:
                nc.vector.quantize_mx(
                    out=page_q[c - 1][:].bitcast(FP8X4), scales=page_sc[c - 1][:],
                    in_=page_bf[:, 4 * BANK * (c - 1) : 4 * BANK * c],
                )
        quantise_w1(1)
        late = sbuf([P, 4 * NP], F32, "late", "page_bf")
        for k in range(HELD_GAINS):
            record_gain(2 + k, late[:, NP * (k + 1) : NP * (k + 2)])
        gp_scale(
            late[:, 0:NP].bitcast(BF16).rearrange("p (g n t) -> p g n t", g=2, t=4),
            wf_raw[:].rearrange("p (g t) n -> p g n t", g=2),
            1.0,
        )

        log_a_tile = sbuf([P, 8 * NP], F32, "log_a", "tab_w")
        log_a = [log_a_tile[:, 4 * NP * g : 4 * NP * (g + 1)] for g in range(2)]
        woven_start = 4 * NP - 2 * WEAVE_CUTS[2]
        woven_first = log_a_tile[:, woven_start : woven_start + 2 * NP].bitcast(BF16)
        proj = {}
        last_bank = {}
        h_q = {1: sbuf([P, NP], U32, "h_q1")}
        h_sc = [sbuf([P, NP], U8, "h_sc%d" % g) for g in range(2)]
        h_bf = {}

        def project(tiles):
            for s in tiles:
                proj[s] = sbuf([P, T2], F32, "proj%d" % s, ("page0", "page2", "page3", "page1")[s % 4])
            for c, s in product(range(4), tiles):
                acc = psum.tile([P, BANK], F32, name="acc_a", tag="bank")
                nc.tensor.matmul_mx(
                    out=acc[:],
                    lhsT=w1_q[s // 4][:, P * (s % 4) : P * (s % 4 + 1)].bitcast(FP8X4),
                    lhsT_scale=w1_sc[:, P * s : P * (s + 1)],
                    rhs=page_q[c][:].bitcast(FP8X4),
                    rhs_scale=page_sc[c][:],
                    start=True,
                    stop=True,
                )
                if c == 3 and s in LAST_BANK_ON_VECTOR:
                    last_bank[s] = acc
                else:
                    nc.scalar.copy(proj[s][:, BANK * c : BANK * (c + 1)], acc[:])

        def empty_last_bank(s):
            if s in LAST_BANK_ON_VECTOR:
                nc.vector.tensor_copy(proj[s][:, 3 * BANK : 4 * BANK], last_bank[s][:])

        def pick(s, lo, hi):
            nc.vector.tensor_copy(plane(log_a, s, lo, hi), proj[s][:].indirect(suspect_list[:, lo // 16 : hi // 16]))

        def energy(s, lo, hi):
            part = plane(log_a, s, lo, hi)
            nc.scalar.activation(part, part, ACT.Square)
            nc.scalar.activation(part, part, ACT.Ln, bias=1.0)

        h_planes = [sbuf([P, 4 * NP], BF16, "h_planes%d" % g, ("tab_sc", "w1_raw1")[g]) for g in range(2)]

        def compare(s, lo, hi):
            nc.vector.scalar_tensor_tensor(
                plane(h_planes, s, lo, hi), plane(log_a, s, lo, hi), gain_col[:, s : s + 1],
                gained_b[s][:, lo:hi], ALU.mult, ALU.subtract,
            )

        def weave(copy, g, lo, hi, parts=1, run=4, woven=None):
            if woven is None:
                woven = sbuf([P, 4 * (hi - lo)], BF16, "h_bf%d_%d" % (g, lo))[:]
            h_bf[g, lo] = woven
            width = (hi - lo) // parts
            for k in range(parts):
                planes = h_planes[g][:].rearrange("p (t n) -> p t n", t=4)[:, :, lo + width * k : lo + width * (k + 1)]
                copy(
                    woven[:, 4 * width * k : 4 * width * (k + 1)].rearrange("p (n i t) -> p n t i", i=run, t=4),
                    planes.rearrange("p t (n i) -> p n t i", i=run),
                )

        def quantise_h(g, lo, hi):
            nc.vector.quantize_mx(
                out=h_q[g][:, lo:hi].bitcast(FP8X4), scales=h_sc[g][:, lo:hi], in_=h_bf[g, lo]
            )

        acc_y = {}

        def alarm_pass(g, lo, hi):
            for h in range(2):
                if g == 0:
                    acc_y[lo, h] = psum.tile([P, BANK], F32, name="acc_y", tag="bank")
                wcols = slice(N * g + P * h, N * g + P * (h + 1))
                nc.tensor.matmul_mx(
                    out=acc_y[lo, h][:, 0 : hi - lo],
                    lhsT=wf_q[:, wcols].bitcast(FP8X4),
                    lhsT_scale=wf_sc[:, wcols],
                    rhs=h_q[g][:, lo:hi].bitcast(FP8X4),
                    rhs_scale=h_sc[g][:, lo:hi],
                    start=(g == 0),
                    stop=(g == 1),
                )

        def store(lo, hi):
            for h in range(2):
                acc = acc_y[lo, h][:, 0 : hi - lo]
                staged = staged_tile[:, NP * h + lo : NP * h + hi]
                if h == 1 and lo >= NP // 2:
                    nc.vector.tensor_scalar_add(staged, acc, minus_thr[:, h : h + 1])
                else:
                    nc.scalar.activation(staged, acc, ACT.Identity, bias=minus_thr[:, h : h + 1])
                nc.sync.dma_start(out[P * h : P * (h + 1), lo:hi], staged)

        project((0, 1))
        for s in range(7):
            if s < 6:
                project((s + 2,))
            empty_last_bank(s + 1 if s else 0)
            pick(s, 0, NP)
            energy(s, 0, NP)
            if s == 5:
                wf_q = sbuf([P, 2 * N], U32, "wf_q", "page2")
                wf_sc = sbuf([P, 2 * N], U8, "wf_sc")
                nc.vector.quantize_mx(
                    out=wf_q[:].bitcast(FP8X4), scales=wf_sc[:], in_=late[:, 0:NP].bitcast(BF16)
                )
            if s == 6:
                h_q[0] = sbuf([P, NP], U32, "h_q0", "page3")
                h_bf[0, 0] = woven_first[:, 0 : 2 * NP]
                h_bf[0, NP // 2] = woven_first[:, 2 * NP : 4 * NP]
                quantise_h(0, 0, NP // 2)
            if s >= 1:
                compare(s - 1, 0, NP)
            if s == 5:
                lo, hi = WEAVE_CUTS[0:2]
                weave(nc.scalar.copy, 0, lo, hi, woven=woven_first[:, 4 * lo : 4 * hi])
            if s in (4, 5):
                lo, hi = WEAVE_CUTS[s - 3 : s - 1]
                weave(gp_cast, 0, lo, hi, 1, 1, woven_first[:, 4 * lo : 4 * hi])
            if 1 <= s <= 3:
                record_gain(s + 4, gained_b[s - 1])
        staged_tile = sbuf([P, 2 * NP], F32, "staged", "wf_raw")
        for chunk in END_CHUNKS:
            pick(7, *chunk)
            energy(7, *chunk)
        compare(6, 0, NP)
        for chunk in END_CHUNKS:
            compare(7, *chunk)
        quarters = [(QUARTER * k, QUARTER * (k + 1)) for k in range(4)]
        weave(nc.scalar.copy, 1, *quarters[0])
        weave(nc.scalar.copy, 1, *quarters[3])
        quantise_h(0, NP // 2, NP)
        for cols in quarters:
            alarm_pass(0, *cols)
        for woven_next, finished in ((1, 0), (2, 1), (None, 3), (None, 2)):
            if woven_next is not None:
                weave(nc.vector.tensor_copy, 1, *quarters[woven_next])
            quantise_h(1, *quarters[finished])
            alarm_pass(1, *quarters[finished])
            store(*quarters[finished])
